import numpy as np
import ml_dtypes


def mxq(x, axis, fmt="e4m3"):
    dtype, down = {"e4m3": (ml_dtypes.float8_e4m3fn, 7), "e5m2": (ml_dtypes.float8_e5m2, 14)}[fmt]
    v = np.moveaxis(np.asarray(x, np.float32).astype(ml_dtypes.bfloat16).astype(np.float64), axis, -1)
    blocks = v.reshape(v.shape[:-1] + (-1, 32))
    amax = np.abs(blocks).max(-1, keepdims=True)
    byte = np.maximum(np.where(amax > 0, np.frexp(amax)[1] - 1 + 127, 0) - down, 1)
    scale = np.exp2(byte - 127.0)
    codes = (blocks / scale).astype(np.float32).astype(dtype).astype(np.float64)
    return np.moveaxis((codes * scale).reshape(v.shape), -1, axis)


WIDE = False


def mx_kscale(k):
    if not WIDE:
        return np.ones(k)
    levels = np.array([10, -10, 5, -5, 0])
    if k % 512:
        return np.exp2(np.random.permutation(np.resize(levels, k // 32))).repeat(32)
    a = np.empty((k // 512, 16))
    for p in range(k // 512):
        a[p, :8] = np.random.permutation(np.resize(levels, 8))
        for g in range(8):
            far = levels[np.abs(levels - a[p, g]) >= 10]
            a[p, g + 8] = far[np.random.randint(len(far))]
    return np.exp2(a.ravel()).repeat(32)


def f64(x):
    return np.asarray(x).astype(np.float64)


def striped(idx):
    return np.tile(idx.reshape(-1, 16).T, (8, 1)).astype(np.uint16)


def unstriped(offs):
    return offs[:16].T.reshape(-1).astype(np.int64)


def pack_weight(w):
    k, n = w.shape
    w = f64(np.asarray(w, np.float32).astype(ml_dtypes.bfloat16)).reshape(k // 32, 32, n)
    amax = np.abs(w).max(1)
    byte = np.clip(np.where(amax > 0, np.frexp(amax)[1] - 1 + 127 - 7, 1), 1, 254)
    scaled = (w * np.exp2(127.0 - byte)[:, None, :]).reshape(k, n).astype(np.float32)
    words = np.ascontiguousarray(scaled.reshape(k // 512, 128, 4, n).transpose(0, 1, 3, 2)).astype(ml_dtypes.float8_e4m3fn).view(np.uint8)
    return words, np.ascontiguousarray(byte.astype(np.uint8).reshape(k // 512, 16, n))


def unpack_weight(words, scales):
    g, p, n, _ = words.shape
    vals = np.ascontiguousarray(words).view(ml_dtypes.float8_e4m3fn).astype(np.float64) * np.repeat(np.exp2(scales.astype(np.float64) - 127.0), 8, axis=1)[..., None]
    return vals.transpose(0, 1, 3, 2).reshape(g * 512, n)


def gelu(v):
    return 0.5 * v * (1.0 + np.tanh(np.sqrt(2.0 / np.pi) * (v + 0.044715 * v**3)))


K, T, S, V, H, G = 512, 2048, 512, 512, 512, 2048


def setup_inputs():
    n = np.random.standard_normal
    s = mx_kscale(K)[:, None]
    u = mx_kscale(H)
    packed_xT = pack_weight(n((K, T)) * s)
    packed_vT = pack_weight(n((H, G)) / np.sqrt(H) / u[:, None])
    return {
        "x_words": packed_xT[0],
        "x_scales": packed_xT[1],
        "w1": (n((K, H)) / np.sqrt(K) / s * u).astype(np.float32),
        "v_words": packed_vT[0],
        "v_scales": packed_vT[1],
        "offs": striped(np.random.permutation(T)[:S]),
        "neg": striped(np.random.permutation(G)[:V]),
    }


def reference(x_words, x_scales, w1, v_words, v_scales, offs, neg):
    xq = unpack_weight(x_words, x_scales)[:, unstriped(offs)]
    h = gelu(mxq(f64(w1), 0, "e4m3").T @ xq)
    v_neg = unpack_weight(v_words, v_scales)[:, unstriped(neg)]
    y = mxq(h, 0, "e4m3").T @ v_neg
    e = np.exp(y - y.max(axis=1, keepdims=True))
    return e / e.sum(axis=1, keepdims=True)

@@ -1,0 +1,144 @@
+from contextlib import ExitStack
+
+import concourse.mybir as mybir
+
+F32 = mybir.dt.float32
+BF16 = mybir.dt.bfloat16
+I32 = mybir.dt.int32
+U32 = mybir.dt.uint32
+U16 = mybir.dt.uint16
+U8 = mybir.dt.uint8
+FP8X4 = mybir.dt.float8_e4m3fn_x4
+ACT = mybir.ActivationFunctionType
+ALU = mybir.AluOpType
+AXIS = mybir.AxisListType
+
+P = 128
+PACK = 4
+STORED = 2048
+PICKED = 512
+HIDDEN = 512
+TILE = 128
+TILES = PICKED // TILE
+HALF = PICKED // 2
+V_ROW = 4
+M_SPLIT = 80
+FLOPS = 2 * 512 * 512 * 512 * 2
+
+
+def tile_picked_zmoco_gelu_p_kernel(tc, x_words, x_scales, w1, v_words, v_scales, offs, neg, out):
+    nc = tc.nc
+    with ExitStack() as ctx:
+        keep = ctx.enter_context(tc.tile_pool(name="keep", bufs=1))
+        psum = ctx.enter_context(tc.psum_pool(name="psum", bufs=1))
+
+        offs_sb = keep.tile([P, PICKED // 16], U16, name="offs_sb")
+        neg_sb = keep.tile([P, PICKED // 16], U16, name="neg_sb")
+        w_raw = keep.tile([P, PACK, HIDDEN], F32, name="w_raw")
+        x_table = keep.tile([P, STORED], I32, name="x_table", align_bytes=64)
+        v_table = keep.tile([P, STORED], I32, name="v_table", align_bytes=64)
+        xs_table = keep.tile([P, STORED], U8, name="xs_table", align_bytes=64)
+        vs_table = keep.tile([P, STORED], U8, name="vs_table", align_bytes=64)
+        warm_in = keep.tile([P, 1], F32, name="warm_in")
+        warm_out = keep.tile([P, 1], F32, name="warm_out")
+
+        nc.vector.memset(xs_table[:].bitcast(I32), 0)
+        nc.vector.memset(vs_table[:].bitcast(I32), 0)
+        nc.gpsimd.memset(warm_in[:], 0.0)
+
+        nc.sync.dma_start(offs_sb[:], offs)
+        nc.sync.dma_start(w_raw[:], w1.rearrange("(p j) c -> p j c", j=PACK))
+        for q in range(4):
+            nc.scalar.dma_start(xs_table[32 * q : 32 * q + 4, :].bitcast(I32), x_scales[0, 4 * q : 4 * q + 4, :].bitcast(I32))
+        nc.sync.dma_start(x_table[:], x_words[0].rearrange("p n t -> p (n t)").bitcast(I32))
+        for q in range(4):
+            nc.gpsimd.dma_start(vs_table[32 * q + V_ROW : 32 * q + V_ROW + 4, :].bitcast(I32), v_scales[0, 4 * q : 4 * q + 4, :].bitcast(I32))
+        nc.sync.dma_start(neg_sb[:], neg)
+        nc.sync.dma_start(v_table[:], v_words[0].rearrange("p n t -> p (n t)").bitcast(I32))
+
+        nc.scalar.activation(warm_out[:], warm_in[:], ACT.Gelu_apprx_tanh)
+
+        xs_picked = keep.tile([P, PICKED], U8, name="xs_picked", align_bytes=64)
+        nc.vector.tensor_copy(xs_picked[:], xs_table[:].indirect(offs_sb[:]))
+
+        w_bf = keep.tile([P, PACK * HIDDEN], BF16, name="w_bf", align_bytes=64)
+        w_dst = w_bf[:].rearrange("p (t m j) -> p m t j", t=PACK, j=PACK)
+        w_src = w_raw[:].rearrange("p j (m t) -> p m t j", t=PACK)
+        nc.vector.tensor_copy(w_dst[:, :M_SPLIT], w_src[:, :M_SPLIT])
+        nc.scalar.activation(w_dst[:, M_SPLIT:], w_src[:, M_SPLIT:], ACT.Copy)
+        w_codes = keep.tile([P, HIDDEN], U32, name="w_codes", align_bytes=64)
+        w_scale = keep.tile([P, HIDDEN], U8, name="w_scale", align_bytes=64)
+        nc.vector.quantize_mx(w_codes[:].bitcast(FP8X4), w_scale[:], w_bf[:])
+
+        x_picked = []
+        for half in range(2):
+            picked = keep.tile([P, HALF], U32, name="x_picked%d" % half, align_bytes=64)
+            cols = slice(half * HALF // 16, (half + 1) * HALF // 16)
+            nc.vector.tensor_copy(picked[:], x_table[:].bitcast(U32).indirect(offs_sb[:, cols]))
+            x_picked.append(picked)
+
+        h_bf = []
+        for n in range(TILES):
+            pre = psum.tile([P, PACK, TILE], F32, name="pre%d" % n)
+            first = (n % 2) * TILE
+            for j in range(PACK):
+                nc.tensor.matmul_mx(
+                    pre[:, j, :],
+                    lhsT=w_codes[:, j * TILE : (j + 1) * TILE].bitcast(FP8X4),
+                    lhsT_scale=w_scale[:, j * TILE : (j + 1) * TILE],
+                    rhs=x_picked[n // 2][:, first : first + TILE].bitcast(FP8X4),
+                    rhs_scale=xs_picked[:, n * TILE : (n + 1) * TILE],
+                    start=True,
+                    stop=True,
+                )
+            h = keep.tile([P, TILE * PACK], BF16, name="h_bf%d" % n, align_bytes=64)
+            nc.scalar.activation(h[:].rearrange("p (n j) -> p n j", j=PACK), pre[:].rearrange("p j n -> p n j"), ACT.Gelu_apprx_tanh)
+            h_bf.append(h)
+
+        vs_picked = keep.tile([P, PICKED], U8, name="vs_picked", align_bytes=64)
+        nc.vector.tensor_copy(vs_picked[:], vs_table[:].indirect(neg_sb[:]))
+        v_picked = keep.tile([P, PICKED], U32, name="v_picked", align_bytes=64)
+        nc.vector.tensor_copy(v_picked[:], v_table[:].bitcast(U32).indirect(neg_sb[:]))
+
+        scores = []
+        for n in range(TILES):
+            h_codes = keep.tile([P, TILE], U32, name="h_codes%d" % n, align_bytes=64)
+            h_scale = keep.tile([P, TILE], U8, name="h_scale%d" % n, align_bytes=64)
+            nc.vector.quantize_mx(h_codes[:].bitcast(FP8X4), h_scale[:], h_bf[n][:])
+            y = psum.tile([P, PICKED], F32, name="y%d" % n)
+            nc.tensor.matmul_mx(
+                y[:],
+                lhsT=h_codes[:].bitcast(FP8X4),
+                lhsT_scale=h_scale[:],
+                rhs=v_picked[:].bitcast(FP8X4),
+                rhs_scale=vs_picked[V_ROW:P, :],
+                start=True,
+                stop=True,
+            )
+            scores.append(y)
+
+        def exponentials(n):
+            neg_max = keep.tile([P, 1], F32, name="neg_max%d" % n)
+            nc.vector.tensor_reduce(neg_max[:], scores[n][:], AXIS.X, ALU.max, negate=True)
+            e = keep.tile([P, PICKED], F32, name="e%d" % n)
+            total = keep.tile([P, 1], F32, name="total%d" % n)
+            nc.scalar.activation(e[:], scores[n][:], ACT.Exp, bias=neg_max[:], accum_out=total[:])
+            return e, total
+
+        def normalise(n, e, total):
+            inv = keep.tile([P, 1], F32, name="inv%d" % n)
+            nc.vector.reciprocal(inv[:], total[:])
+            res = keep.tile([P, PICKED], F32, name="res%d" % n)
+            if n < 2:
+                nc.gpsimd.tensor_scalar(res[:], e[:], inv[:], 0.0, ALU.mult, ALU.add)
+            else:
+                nc.vector.tensor_scalar(res[:], e[:], inv[:], None, ALU.mult)
+            nc.sync.dma_start(out[n * TILE : (n + 1) * TILE, :], res[:])
+
+        last = None
+        for n in range(TILES):
+            this = exponentials(n)
+            if n > 0:
+                normalise(n - 1, *last)
+            last = this
+        normalise(TILES - 1, *last)

@@ -22,7 +22,7 @@ TILE = 128
 TILES = PICKED // TILE
 HALF = PICKED // 2
 V_ROW = 4
-M_SPLIT = 80
+M_SPLIT = 48
 FLOPS = 2 * 512 * 512 * 512 * 2
 
 
@@ -35,58 +35,55 @@ def tile_picked_zmoco_gelu_p_kernel(tc, x_words, x_scales, w1, v_words, v_scales
         offs_sb = keep.tile([P, PICKED // 16], U16, name="offs_sb")
         neg_sb = keep.tile([P, PICKED // 16], U16, name="neg_sb")
         w_raw = keep.tile([P, PACK, HIDDEN], F32, name="w_raw")
-        x_table = keep.tile([P, STORED], I32, name="x_table", align_bytes=64)
-        v_table = keep.tile([P, STORED], I32, name="v_table", align_bytes=64)
-        xs_table = keep.tile([P, STORED], U8, name="xs_table", align_bytes=64)
-        vs_table = keep.tile([P, STORED], U8, name="vs_table", align_bytes=64)
-        warm_in = keep.tile([P, 1], F32, name="warm_in")
+        x_table = keep.tile([P, STORED], I32, name="x_table", tag="slot_x", align_bytes=64)
+        xs_table = keep.tile([P, STORED], U8, name="xs_table", tag="slot_xs", align_bytes=64)
+        vs_table = keep.tile([P, STORED], U8, name="vs_table", tag="slot_vs", align_bytes=64)
+        warm_in = keep.tile([P, 1], F32, name="warm_in", tag="slot_v", align_bytes=64)
         warm_out = keep.tile([P, 1], F32, name="warm_out")
 
         nc.vector.memset(xs_table[:].bitcast(I32), 0)
-        nc.vector.memset(vs_table[:].bitcast(I32), 0)
-        nc.gpsimd.memset(warm_in[:], 0.0)
+        nc.vector.memset(warm_in[:], 0.0)
+        nc.gpsimd.memset(vs_table[:].bitcast(I32), 0)
 
-        nc.sync.dma_start(offs_sb[:], offs)
         nc.sync.dma_start(w_raw[:], w1.rearrange("(p j) c -> p j c", j=PACK))
+        nc.sync.dma_start(offs_sb[:], offs)
         for q in range(4):
             nc.scalar.dma_start(xs_table[32 * q : 32 * q + 4, :].bitcast(I32), x_scales[0, 4 * q : 4 * q + 4, :].bitcast(I32))
+        nc.sync.dma_start(neg_sb[:], neg)
         nc.sync.dma_start(x_table[:], x_words[0].rearrange("p n t -> p (n t)").bitcast(I32))
         for q in range(4):
             nc.gpsimd.dma_start(vs_table[32 * q + V_ROW : 32 * q + V_ROW + 4, :].bitcast(I32), v_scales[0, 4 * q : 4 * q + 4, :].bitcast(I32))
-        nc.sync.dma_start(neg_sb[:], neg)
-        nc.sync.dma_start(v_table[:], v_words[0].rearrange("p n t -> p (n t)").bitcast(I32))
 
         nc.scalar.activation(warm_out[:], warm_in[:], ACT.Gelu_apprx_tanh)
+        v_table = keep.tile([P, STORED], I32, name="v_table", tag="slot_v", align_bytes=64)
+        nc.sync.dma_start(v_table[:], v_words[0].rearrange("p n t -> p (n t)").bitcast(I32))
 
         xs_picked = keep.tile([P, PICKED], U8, name="xs_picked", align_bytes=64)
         nc.vector.tensor_copy(xs_picked[:], xs_table[:].indirect(offs_sb[:]))
 
-        w_bf = keep.tile([P, PACK * HIDDEN], BF16, name="w_bf", align_bytes=64)
+        w_bf = keep.tile([P, PACK * HIDDEN], BF16, name="w_bf", tag="slot_w", align_bytes=64)
         w_dst = w_bf[:].rearrange("p (t m j) -> p m t j", t=PACK, j=PACK)
         w_src = w_raw[:].rearrange("p j (m t) -> p m t j", t=PACK)
         nc.vector.tensor_copy(w_dst[:, :M_SPLIT], w_src[:, :M_SPLIT])
         nc.scalar.activation(w_dst[:, M_SPLIT:], w_src[:, M_SPLIT:], ACT.Copy)
-        w_codes = keep.tile([P, HIDDEN], U32, name="w_codes", align_bytes=64)
+        w_codes = keep.tile([P, HIDDEN], U32, name="w_codes", tag="slot_xs", align_bytes=64)
         w_scale = keep.tile([P, HIDDEN], U8, name="w_scale", align_bytes=64)
         nc.vector.quantize_mx(w_codes[:].bitcast(FP8X4), w_scale[:], w_bf[:])
 
-        x_picked = []
+        x_picked = keep.tile([P, PICKED], U32, name="x_picked", tag="slot_w", align_bytes=64)
         for half in range(2):
-            picked = keep.tile([P, HALF], U32, name="x_picked%d" % half, align_bytes=64)
             cols = slice(half * HALF // 16, (half + 1) * HALF // 16)
-            nc.vector.tensor_copy(picked[:], x_table[:].bitcast(U32).indirect(offs_sb[:, cols]))
-            x_picked.append(picked)
+            nc.vector.tensor_copy(x_picked[:, half * HALF : (half + 1) * HALF], x_table[:].bitcast(U32).indirect(offs_sb[:, cols]))
 
         h_bf = []
         for n in range(TILES):
             pre = psum.tile([P, PACK, TILE], F32, name="pre%d" % n)
-            first = (n % 2) * TILE
             for j in range(PACK):
                 nc.tensor.matmul_mx(
                     pre[:, j, :],
                     lhsT=w_codes[:, j * TILE : (j + 1) * TILE].bitcast(FP8X4),
                     lhsT_scale=w_scale[:, j * TILE : (j + 1) * TILE],
-                    rhs=x_picked[n // 2][:, first : first + TILE].bitcast(FP8X4),
+                    rhs=x_picked[:, n * TILE : (n + 1) * TILE].bitcast(FP8X4),
                     rhs_scale=xs_picked[:, n * TILE : (n + 1) * TILE],
                     start=True,
                     stop=True,
@@ -95,20 +92,21 @@ def tile_picked_zmoco_gelu_p_kernel(tc, x_words, x_scales, w1, v_words, v_scales
             nc.scalar.activation(h[:].rearrange("p (n j) -> p n j", j=PACK), pre[:].rearrange("p j n -> p n j"), ACT.Gelu_apprx_tanh)
             h_bf.append(h)
 
-        vs_picked = keep.tile([P, PICKED], U8, name="vs_picked", align_bytes=64)
+        vs_picked = keep.tile([P, PICKED], U8, name="vs_picked", tag="slot_x", align_bytes=64)
         nc.vector.tensor_copy(vs_picked[:], vs_table[:].indirect(neg_sb[:]))
-        v_picked = keep.tile([P, PICKED], U32, name="v_picked", align_bytes=64)
+        v_picked = keep.tile([P, PICKED], U32, name="v_picked", tag="slot_vs", align_bytes=64)
         nc.vector.tensor_copy(v_picked[:], v_table[:].bitcast(U32).indirect(neg_sb[:]))
 
         scores = []
+        h_codes_all = keep.tile([P, PICKED], U32, name="h_codes_all", tag="slot_v", align_bytes=64)
         for n in range(TILES):
-            h_codes = keep.tile([P, TILE], U32, name="h_codes%d" % n, align_bytes=64)
+            h_codes = h_codes_all[:, n * TILE : (n + 1) * TILE]
             h_scale = keep.tile([P, TILE], U8, name="h_scale%d" % n, align_bytes=64)
-            nc.vector.quantize_mx(h_codes[:].bitcast(FP8X4), h_scale[:], h_bf[n][:])
+            nc.vector.quantize_mx(h_codes.bitcast(FP8X4), h_scale[:], h_bf[n][:])
             y = psum.tile([P, PICKED], F32, name="y%d" % n)
             nc.tensor.matmul_mx(
                 y[:],
-                lhsT=h_codes[:].bitcast(FP8X4),
+                lhsT=h_codes.bitcast(FP8X4),
                 lhsT_scale=h_scale[:],
                 rhs=v_picked[:].bitcast(FP8X4),
                 rhs_scale=vs_picked[V_ROW:P, :],
@@ -129,10 +127,7 @@ def tile_picked_zmoco_gelu_p_kernel(tc, x_words, x_scales, w1, v_words, v_scales
             inv = keep.tile([P, 1], F32, name="inv%d" % n)
             nc.vector.reciprocal(inv[:], total[:])
             res = keep.tile([P, PICKED], F32, name="res%d" % n)
-            if n < 2:
-                nc.gpsimd.tensor_scalar(res[:], e[:], inv[:], 0.0, ALU.mult, ALU.add)
-            else:
-                nc.vector.tensor_scalar(res[:], e[:], inv[:], None, ALU.mult)
+            nc.vector.tensor_scalar(res[:], e[:], inv[:], None, ALU.mult)
             nc.sync.dma_start(out[n * TILE : (n + 1) * TILE, :], res[:])
 
         last = None

@@ -22,7 +22,7 @@ TILE = 128
 TILES = PICKED // TILE
 HALF = PICKED // 2
 V_ROW = 4
-M_SPLIT = 48
+M_SPLIT = 40
 FLOPS = 2 * 512 * 512 * 512 * 2
 
 
@@ -30,38 +30,39 @@ def tile_picked_zmoco_gelu_p_kernel(tc, x_words, x_scales, w1, v_words, v_scales
     nc = tc.nc
     with ExitStack() as ctx:
         keep = ctx.enter_context(tc.tile_pool(name="keep", bufs=1))
+        late = ctx.enter_context(tc.tile_pool(name="late", bufs=1))
         psum = ctx.enter_context(tc.psum_pool(name="psum", bufs=1))
 
         offs_sb = keep.tile([P, PICKED // 16], U16, name="offs_sb")
         neg_sb = keep.tile([P, PICKED // 16], U16, name="neg_sb")
         w_raw = keep.tile([P, PACK, HIDDEN], F32, name="w_raw")
-        x_table = keep.tile([P, STORED], I32, name="x_table", tag="slot_x", align_bytes=64)
+        x_table = keep.tile([P, STORED], I32, name="x_table", align_bytes=64)
         xs_table = keep.tile([P, STORED], U8, name="xs_table", tag="slot_xs", align_bytes=64)
         vs_table = keep.tile([P, STORED], U8, name="vs_table", tag="slot_vs", align_bytes=64)
-        warm_in = keep.tile([P, 1], F32, name="warm_in", tag="slot_v", align_bytes=64)
+        warm_in = keep.tile([P, 1], F32, name="warm_in")
         warm_out = keep.tile([P, 1], F32, name="warm_out")
 
+        v_table = late.tile([P, STORED], I32, name="v_table", offset=0, align_bytes=64)
         nc.vector.memset(xs_table[:].bitcast(I32), 0)
-        nc.vector.memset(warm_in[:], 0.0)
-        nc.gpsimd.memset(vs_table[:].bitcast(I32), 0)
+        nc.gpsimd.memset(warm_in[:], 0.0)
+        nc.vector.memset(vs_table[:].bitcast(I32), 0)
 
         nc.sync.dma_start(w_raw[:], w1.rearrange("(p j) c -> p j c", j=PACK))
         nc.sync.dma_start(offs_sb[:], offs)
         for q in range(4):
-            nc.scalar.dma_start(xs_table[32 * q : 32 * q + 4, :].bitcast(I32), x_scales[0, 4 * q : 4 * q + 4, :].bitcast(I32))
-        nc.sync.dma_start(neg_sb[:], neg)
+            nc.sync.dma_start(xs_table[32 * q : 32 * q + 4, :].bitcast(I32), x_scales[0, 4 * q : 4 * q + 4, :].bitcast(I32))
         nc.sync.dma_start(x_table[:], x_words[0].rearrange("p n t -> p (n t)").bitcast(I32))
+        nc.sync.dma_start(neg_sb[:], neg)
         for q in range(4):
-            nc.gpsimd.dma_start(vs_table[32 * q + V_ROW : 32 * q + V_ROW + 4, :].bitcast(I32), v_scales[0, 4 * q : 4 * q + 4, :].bitcast(I32))
+            nc.sync.dma_start(vs_table[32 * q + V_ROW : 32 * q + V_ROW + 4, :].bitcast(I32), v_scales[0, 4 * q : 4 * q + 4, :].bitcast(I32))
+        nc.sync.dma_start(v_table[:], v_words[0].rearrange("p n t -> p (n t)").bitcast(I32))
 
         nc.scalar.activation(warm_out[:], warm_in[:], ACT.Gelu_apprx_tanh)
-        v_table = keep.tile([P, STORED], I32, name="v_table", tag="slot_v", align_bytes=64)
-        nc.sync.dma_start(v_table[:], v_words[0].rearrange("p n t -> p (n t)").bitcast(I32))
 
         xs_picked = keep.tile([P, PICKED], U8, name="xs_picked", align_bytes=64)
         nc.vector.tensor_copy(xs_picked[:], xs_table[:].indirect(offs_sb[:]))
 
-        w_bf = keep.tile([P, PACK * HIDDEN], BF16, name="w_bf", tag="slot_w", align_bytes=64)
+        w_bf = keep.tile([P, PACK * HIDDEN], BF16, name="w_bf", align_bytes=64)
         w_dst = w_bf[:].rearrange("p (t m j) -> p m t j", t=PACK, j=PACK)
         w_src = w_raw[:].rearrange("p j (m t) -> p m t j", t=PACK)
         nc.vector.tensor_copy(w_dst[:, :M_SPLIT], w_src[:, :M_SPLIT])
@@ -70,7 +71,7 @@ def tile_picked_zmoco_gelu_p_kernel(tc, x_words, x_scales, w1, v_words, v_scales
         w_scale = keep.tile([P, HIDDEN], U8, name="w_scale", align_bytes=64)
         nc.vector.quantize_mx(w_codes[:].bitcast(FP8X4), w_scale[:], w_bf[:])
 
-        x_picked = keep.tile([P, PICKED], U32, name="x_picked", tag="slot_w", align_bytes=64)
+        x_picked = keep.tile([P, PICKED], U32, name="x_picked", align_bytes=64)
         for half in range(2):
             cols = slice(half * HALF // 16, (half + 1) * HALF // 16)
             nc.vector.tensor_copy(x_picked[:, half * HALF : (half + 1) * HALF], x_table[:].bitcast(U32).indirect(offs_sb[:, cols]))
@@ -92,48 +93,66 @@ def tile_picked_zmoco_gelu_p_kernel(tc, x_words, x_scales, w1, v_words, v_scales
             nc.scalar.activation(h[:].rearrange("p (n j) -> p n j", j=PACK), pre[:].rearrange("p j n -> p n j"), ACT.Gelu_apprx_tanh)
             h_bf.append(h)
 
-        vs_picked = keep.tile([P, PICKED], U8, name="vs_picked", tag="slot_x", align_bytes=64)
+        vs_picked = keep.tile([P, PICKED], U8, name="vs_picked", align_bytes=64)
         nc.vector.tensor_copy(vs_picked[:], vs_table[:].indirect(neg_sb[:]))
-        v_picked = keep.tile([P, PICKED], U32, name="v_picked", tag="slot_vs", align_bytes=64)
-        nc.vector.tensor_copy(v_picked[:], v_table[:].bitcast(U32).indirect(neg_sb[:]))
 
-        scores = []
-        h_codes_all = keep.tile([P, PICKED], U32, name="h_codes_all", tag="slot_v", align_bytes=64)
-        for n in range(TILES):
-            h_codes = h_codes_all[:, n * TILE : (n + 1) * TILE]
-            h_scale = keep.tile([P, TILE], U8, name="h_scale%d" % n, align_bytes=64)
-            nc.vector.quantize_mx(h_codes.bitcast(FP8X4), h_scale[:], h_bf[n][:])
-            y = psum.tile([P, PICKED], F32, name="y%d" % n)
+        def quantise_hidden(n):
+            if n == 0:
+                codes = keep.tile([P, TILE], U32, name="h_codes0", tag="slot_vs", align_bytes=64)
+            else:
+                codes = late.tile([P, TILE], U32, name="h_codes%d" % n, offset=n * TILE * 4, align_bytes=64)
+            scale = keep.tile([P, TILE], U8, name="h_scale%d" % n, align_bytes=64)
+            nc.vector.quantize_mx(codes[:].bitcast(FP8X4), scale[:], h_bf[n][:])
+            return codes, scale
+
+        def score(y, hidden, cols):
+            codes, scale = hidden
             nc.tensor.matmul_mx(
-                y[:],
-                lhsT=h_codes.bitcast(FP8X4),
-                lhsT_scale=h_scale[:],
-                rhs=v_picked[:].bitcast(FP8X4),
-                rhs_scale=vs_picked[V_ROW:P, :],
+                y[:, cols],
+                lhsT=codes[:].bitcast(FP8X4),
+                lhsT_scale=scale[:],
+                rhs=v_picked[:, cols].bitcast(FP8X4),
+                rhs_scale=vs_picked[V_ROW:P, cols],
                 start=True,
                 stop=True,
             )
-            scores.append(y)
+
+        scores = [psum.tile([P, PICKED], F32, name="y%d" % n) for n in range(TILES)]
+        hidden = quantise_hidden(0)
+        v_picked = keep.tile([P, PICKED], U32, name="v_picked", align_bytes=64)
+        for half in range(2):
+            entries = slice(half * HALF // 16, (half + 1) * HALF // 16)
+            cols = slice(half * HALF, (half + 1) * HALF)
+            nc.vector.tensor_copy(v_picked[:, cols], v_table[:].bitcast(U32).indirect(neg_sb[:, entries]))
+            score(scores[0], hidden, cols)
+        for n in range(1, TILES):
+            score(scores[n], quantise_hidden(n), slice(0, PICKED))
 
         def exponentials(n):
-            neg_max = keep.tile([P, 1], F32, name="neg_max%d" % n)
+            neg_max = keep.tile([P, 1], F32, name="neg_max%d" % n, tag="neg_max%d" % (n % 3))
             nc.vector.tensor_reduce(neg_max[:], scores[n][:], AXIS.X, ALU.max, negate=True)
             e = keep.tile([P, PICKED], F32, name="e%d" % n)
             total = keep.tile([P, 1], F32, name="total%d" % n)
             nc.scalar.activation(e[:], scores[n][:], ACT.Exp, bias=neg_max[:], accum_out=total[:])
             return e, total
 
-        def normalise(n, e, total):
+        def inverse(n, total):
             inv = keep.tile([P, 1], F32, name="inv%d" % n)
             nc.vector.reciprocal(inv[:], total[:])
+            return inv
+
+        def normalise(n, e, inv):
             res = keep.tile([P, PICKED], F32, name="res%d" % n)
             nc.vector.tensor_scalar(res[:], e[:], inv[:], None, ALU.mult)
             nc.sync.dma_start(out[n * TILE : (n + 1) * TILE, :], res[:])
 
-        last = None
-        for n in range(TILES):
-            this = exponentials(n)
-            if n > 0:
-                normalise(n - 1, *last)
-            last = this
-        normalise(TILES - 1, *last)
+        e0, total0 = exponentials(0)
+        e1, total1 = exponentials(1)
+        e2, total2 = exponentials(2)
+        inv0 = inverse(0, total0)
+        e3, total3 = exponentials(3)
+        inv1 = inverse(1, total1)
+        normalise(0, e0, inv0)
+        normalise(1, e1, inv1)
+        normalise(2, e2, inverse(2, total2))
+        normalise(3, e3, inverse(3, total3))

@@ -22,7 +22,7 @@ TILE = 128
 TILES = PICKED // TILE
 HALF = PICKED // 2
 V_ROW = 4
-M_SPLIT = 40
+M_SPLIT = 52
 FLOPS = 2 * 512 * 512 * 512 * 2
 
 
@@ -50,11 +50,11 @@ def tile_picked_zmoco_gelu_p_kernel(tc, x_words, x_scales, w1, v_words, v_scales
         nc.sync.dma_start(w_raw[:], w1.rearrange("(p j) c -> p j c", j=PACK))
         nc.sync.dma_start(offs_sb[:], offs)
         for q in range(4):
-            nc.sync.dma_start(xs_table[32 * q : 32 * q + 4, :].bitcast(I32), x_scales[0, 4 * q : 4 * q + 4, :].bitcast(I32))
+            nc.sync.dma_start(xs_table[q:P:32, :].bitcast(I32), x_scales[0, q:16:4, :].bitcast(I32))
         nc.sync.dma_start(x_table[:], x_words[0].rearrange("p n t -> p (n t)").bitcast(I32))
         nc.sync.dma_start(neg_sb[:], neg)
         for q in range(4):
-            nc.sync.dma_start(vs_table[32 * q + V_ROW : 32 * q + V_ROW + 4, :].bitcast(I32), v_scales[0, 4 * q : 4 * q + 4, :].bitcast(I32))
+            nc.sync.dma_start(vs_table[V_ROW + q : P : 32, :].bitcast(I32), v_scales[0, q:16:4, :].bitcast(I32))
         nc.sync.dma_start(v_table[:], v_words[0].rearrange("p n t -> p (n t)").bitcast(I32))
 
         nc.scalar.activation(warm_out[:], warm_in[:], ACT.Gelu_apprx_tanh)

@@ -143,8 +143,17 @@ def tile_picked_zmoco_gelu_p_kernel(tc, x_words, x_scales, w1, v_words, v_scales
 
         def normalise(n, e, inv):
             res = keep.tile([P, PICKED], F32, name="res%d" % n)
-            nc.vector.tensor_scalar(res[:], e[:], inv[:], None, ALU.mult)
-            nc.sync.dma_start(out[n * TILE : (n + 1) * TILE, :], res[:])
+            if n in (0, TILES - 1):
+                for half in range(2):
+                    cols = slice(half * HALF, (half + 1) * HALF)
+                    if n == 0 and half == 0:
+                        nc.gpsimd.tensor_scalar(res[:, cols], e[:, cols], inv[:], 0.0, ALU.mult, ALU.add)
+                    else:
+                        nc.vector.tensor_scalar(res[:, cols], e[:, cols], inv[:], None, ALU.mult)
+                    nc.sync.dma_start(out[n * TILE : (n + 1) * TILE, cols], res[:, cols])
+            else:
+                nc.vector.tensor_scalar(res[:], e[:], inv[:], None, ALU.mult)
+                nc.sync.dma_start(out[n * TILE : (n + 1) * TILE, :], res[:])
 
         e0, total0 = exponentials(0)
         e1, total1 = exponentials(1)

@@ -21,8 +21,9 @@ HIDDEN = 512
 TILE = 128
 TILES = PICKED // TILE
 HALF = PICKED // 2
-V_ROW = 4
-M_SPLIT = 52
+SPREAD = 8
+V_FIRST = 4
+M_SPLIT = 68
 FLOPS = 2 * 512 * 512 * 512 * 2
 
 
@@ -37,37 +38,52 @@ def tile_picked_zmoco_gelu_p_kernel(tc, x_words, x_scales, w1, v_words, v_scales
         neg_sb = keep.tile([P, PICKED // 16], U16, name="neg_sb")
         w_raw = keep.tile([P, PACK, HIDDEN], F32, name="w_raw")
         x_table = keep.tile([P, STORED], I32, name="x_table", align_bytes=64)
-        xs_table = keep.tile([P, STORED], U8, name="xs_table", tag="slot_xs", align_bytes=64)
-        vs_table = keep.tile([P, STORED], U8, name="vs_table", tag="slot_vs", align_bytes=64)
+        xs_table = keep.tile([P, STORED], U8, name="xs_table", align_bytes=64)
+        vs_table = keep.tile([P, STORED], U8, name="vs_table", align_bytes=64)
+        xs_plane = keep.tile([P, PICKED], U8, name="xs_plane", align_bytes=64)
+        vs_plane = keep.tile([P, PICKED], U8, name="vs_plane", align_bytes=64)
         warm_in = keep.tile([P, 1], F32, name="warm_in")
         warm_out = keep.tile([P, 1], F32, name="warm_out")
-
         v_table = late.tile([P, STORED], I32, name="v_table", offset=0, align_bytes=64)
+
         nc.vector.memset(xs_table[:].bitcast(I32), 0)
         nc.gpsimd.memset(warm_in[:], 0.0)
         nc.vector.memset(vs_table[:].bitcast(I32), 0)
+        nc.vector.memset(xs_plane[:].bitcast(I32), 0)
+        nc.vector.memset(vs_plane[:].bitcast(I32), 0)
 
-        nc.sync.dma_start(w_raw[:], w1.rearrange("(p j) c -> p j c", j=PACK))
+        w_rows = w1.rearrange("(p j) c -> p j c", j=PACK)
+        nc.sync.dma_start(w_raw[:, :1], w_rows[:, :1])
         nc.sync.dma_start(offs_sb[:], offs)
-        for q in range(4):
-            nc.sync.dma_start(xs_table[q:P:32, :].bitcast(I32), x_scales[0, q:16:4, :].bitcast(I32))
-        nc.sync.dma_start(x_table[:], x_words[0].rearrange("p n t -> p (n t)").bitcast(I32))
         nc.sync.dma_start(neg_sb[:], neg)
-        for q in range(4):
-            nc.sync.dma_start(vs_table[V_ROW + q : P : 32, :].bitcast(I32), v_scales[0, q:16:4, :].bitcast(I32))
-        nc.sync.dma_start(v_table[:], v_words[0].rearrange("p n t -> p (n t)").bitcast(I32))
+        nc.sync.dma_start(xs_table[0:P:SPREAD, :].bitcast(I32), x_scales[0].bitcast(I32))
+        nc.sync.dma_start(w_raw[:, 1:2], w_rows[:, 1:2])
+        nc.sync.dma_start(vs_table[V_FIRST:P:SPREAD, :].bitcast(I32), v_scales[0].bitcast(I32))
+        nc.sync.dma_start(w_raw[:, 2:], w_rows[:, 2:])
+        nc.sync.dma_start(x_table[:], x_words[0].rearrange("p n t -> p (n t)").bitcast(I32))
 
         nc.scalar.activation(warm_out[:], warm_in[:], ACT.Gelu_apprx_tanh)
 
+        def place(plane, picked, first):
+            for r in range(4):
+                nc.sync.dma_start(plane[r:P:32, :].bitcast(I32), picked[first + SPREAD * r : P : 32, :].bitcast(I32))
+
         xs_picked = keep.tile([P, PICKED], U8, name="xs_picked", align_bytes=64)
         nc.vector.tensor_copy(xs_picked[:], xs_table[:].indirect(offs_sb[:]))
+        place(xs_plane, xs_picked, 0)
+        nc.sync.dma_start(v_table[:], v_words[0].rearrange("p n t -> p (n t)").bitcast(I32))
+
+        vs_picked = keep.tile([P, PICKED], U8, name="vs_picked", align_bytes=64)
+        nc.vector.tensor_copy(vs_picked[:], vs_table[:].indirect(neg_sb[:]))
+        place(vs_plane, vs_picked, V_FIRST)
 
         w_bf = keep.tile([P, PACK * HIDDEN], BF16, name="w_bf", align_bytes=64)
         w_dst = w_bf[:].rearrange("p (t m j) -> p m t j", t=PACK, j=PACK)
         w_src = w_raw[:].rearrange("p j (m t) -> p m t j", t=PACK)
         nc.vector.tensor_copy(w_dst[:, :M_SPLIT], w_src[:, :M_SPLIT])
         nc.scalar.activation(w_dst[:, M_SPLIT:], w_src[:, M_SPLIT:], ACT.Copy)
-        w_codes = keep.tile([P, HIDDEN], U32, name="w_codes", tag="slot_xs", align_bytes=64)
+
+        w_codes = keep.tile([P, HIDDEN], U32, name="w_codes", align_bytes=64)
         w_scale = keep.tile([P, HIDDEN], U8, name="w_scale", align_bytes=64)
         nc.vector.quantize_mx(w_codes[:].bitcast(FP8X4), w_scale[:], w_bf[:])
 
@@ -85,7 +101,7 @@ def tile_picked_zmoco_gelu_p_kernel(tc, x_words, x_scales, w1, v_words, v_scales
                     lhsT=w_codes[:, j * TILE : (j + 1) * TILE].bitcast(FP8X4),
                     lhsT_scale=w_scale[:, j * TILE : (j + 1) * TILE],
                     rhs=x_picked[:, n * TILE : (n + 1) * TILE].bitcast(FP8X4),
-                    rhs_scale=xs_picked[:, n * TILE : (n + 1) * TILE],
+                    rhs_scale=xs_plane[:, n * TILE : (n + 1) * TILE],
                     start=True,
                     stop=True,
                 )
@@ -93,75 +109,42 @@ def tile_picked_zmoco_gelu_p_kernel(tc, x_words, x_scales, w1, v_words, v_scales
             nc.scalar.activation(h[:].rearrange("p (n j) -> p n j", j=PACK), pre[:].rearrange("p j n -> p n j"), ACT.Gelu_apprx_tanh)
             h_bf.append(h)
 
-        vs_picked = keep.tile([P, PICKED], U8, name="vs_picked", align_bytes=64)
-        nc.vector.tensor_copy(vs_picked[:], vs_table[:].indirect(neg_sb[:]))
+        v_picked = keep.tile([P, PICKED], U32, name="v_picked", align_bytes=64)
+        nc.vector.tensor_copy(v_picked[:], v_table[:].bitcast(U32).indirect(neg_sb[:]))
 
-        def quantise_hidden(n):
-            if n == 0:
-                codes = keep.tile([P, TILE], U32, name="h_codes0", tag="slot_vs", align_bytes=64)
-            else:
-                codes = late.tile([P, TILE], U32, name="h_codes%d" % n, offset=n * TILE * 4, align_bytes=64)
+        scores = []
+        for n in range(TILES):
+            codes = late.tile([P, TILE], U32, name="h_codes%d" % n, offset=n * TILE * 4, align_bytes=64)
             scale = keep.tile([P, TILE], U8, name="h_scale%d" % n, align_bytes=64)
             nc.vector.quantize_mx(codes[:].bitcast(FP8X4), scale[:], h_bf[n][:])
-            return codes, scale
-
-        def score(y, hidden, cols):
-            codes, scale = hidden
+            y = psum.tile([P, PICKED], F32, name="y%d" % n)
             nc.tensor.matmul_mx(
-                y[:, cols],
+                y[:],
                 lhsT=codes[:].bitcast(FP8X4),
                 lhsT_scale=scale[:],
-                rhs=v_picked[:, cols].bitcast(FP8X4),
-                rhs_scale=vs_picked[V_ROW:P, cols],
+                rhs=v_picked[:].bitcast(FP8X4),
+                rhs_scale=vs_plane[:],
                 start=True,
                 stop=True,
             )
+            scores.append(y)
 
-        scores = [psum.tile([P, PICKED], F32, name="y%d" % n) for n in range(TILES)]
-        hidden = quantise_hidden(0)
-        v_picked = keep.tile([P, PICKED], U32, name="v_picked", align_bytes=64)
-        for half in range(2):
-            entries = slice(half * HALF // 16, (half + 1) * HALF // 16)
-            cols = slice(half * HALF, (half + 1) * HALF)
-            nc.vector.tensor_copy(v_picked[:, cols], v_table[:].bitcast(U32).indirect(neg_sb[:, entries]))
-            score(scores[0], hidden, cols)
-        for n in range(1, TILES):
-            score(scores[n], quantise_hidden(n), slice(0, PICKED))
-
-        def exponentials(n):
-            neg_max = keep.tile([P, 1], F32, name="neg_max%d" % n, tag="neg_max%d" % (n % 3))
+        exps = []
+        for n in range(TILES):
+            neg_max = keep.tile([P, 1], F32, name="neg_max%d" % n)
             nc.vector.tensor_reduce(neg_max[:], scores[n][:], AXIS.X, ALU.max, negate=True)
             e = keep.tile([P, PICKED], F32, name="e%d" % n)
             total = keep.tile([P, 1], F32, name="total%d" % n)
             nc.scalar.activation(e[:], scores[n][:], ACT.Exp, bias=neg_max[:], accum_out=total[:])
-            return e, total
+            exps.append((e, total))
 
-        def inverse(n, total):
+        for n in range(TILES):
+            e, total = exps[n]
             inv = keep.tile([P, 1], F32, name="inv%d" % n)
             nc.vector.reciprocal(inv[:], total[:])
-            return inv
-
-        def normalise(n, e, inv):
             res = keep.tile([P, PICKED], F32, name="res%d" % n)
-            if n in (0, TILES - 1):
-                for half in range(2):
-                    cols = slice(half * HALF, (half + 1) * HALF)
-                    if n == 0 and half == 0:
-                        nc.gpsimd.tensor_scalar(res[:, cols], e[:, cols], inv[:], 0.0, ALU.mult, ALU.add)
-                    else:
-                        nc.vector.tensor_scalar(res[:, cols], e[:, cols], inv[:], None, ALU.mult)
-                    nc.sync.dma_start(out[n * TILE : (n + 1) * TILE, cols], res[:, cols])
-            else:
-                nc.vector.tensor_scalar(res[:], e[:], inv[:], None, ALU.mult)
-                nc.sync.dma_start(out[n * TILE : (n + 1) * TILE, :], res[:])
-
-        e0, total0 = exponentials(0)
-        e1, total1 = exponentials(1)
-        e2, total2 = exponentials(2)
-        inv0 = inverse(0, total0)
-        e3, total3 = exponentials(3)
-        inv1 = inverse(1, total1)
-        normalise(0, e0, inv0)
-        normalise(1, e1, inv1)
-        normalise(2, e2, inverse(2, total2))
-        normalise(3, e3, inverse(3, total3))
+            pieces = 2 if n in (0, TILES - 1) else 1
+            for piece in range(pieces):
+                cols = slice(piece * PICKED // pieces, (piece + 1) * PICKED // pieces)
+                nc.vector.tensor_scalar(res[:, cols], e[:, cols], inv[:], None, ALU.mult)
+                nc.sync.dma_start(out[n * TILE : (n + 1) * TILE, cols], res[:, cols])

@@ -110,24 +110,37 @@ def tile_picked_zmoco_gelu_p_kernel(tc, x_words, x_scales, w1, v_words, v_scales
             h_bf.append(h)
 
         v_picked = keep.tile([P, PICKED], U32, name="v_picked", align_bytes=64)
-        nc.vector.tensor_copy(v_picked[:], v_table[:].bitcast(U32).indirect(neg_sb[:]))
 
-        scores = []
-        for n in range(TILES):
-            codes = late.tile([P, TILE], U32, name="h_codes%d" % n, offset=n * TILE * 4, align_bytes=64)
+        def quantise_hidden(n):
+            if n == 0:
+                codes = keep.tile([P, TILE], U32, name="h_codes0", align_bytes=64)
+            else:
+                codes = late.tile([P, TILE], U32, name="h_codes%d" % n, offset=n * TILE * 4, align_bytes=64)
             scale = keep.tile([P, TILE], U8, name="h_scale%d" % n, align_bytes=64)
             nc.vector.quantize_mx(codes[:].bitcast(FP8X4), scale[:], h_bf[n][:])
-            y = psum.tile([P, PICKED], F32, name="y%d" % n)
+            return codes, scale
+
+        def score(y, hidden, cols):
+            codes, scale = hidden
             nc.tensor.matmul_mx(
-                y[:],
+                y[:, cols],
                 lhsT=codes[:].bitcast(FP8X4),
                 lhsT_scale=scale[:],
-                rhs=v_picked[:].bitcast(FP8X4),
-                rhs_scale=vs_plane[:],
+                rhs=v_picked[:, cols].bitcast(FP8X4),
+                rhs_scale=vs_plane[:, cols],
                 start=True,
                 stop=True,
             )
-            scores.append(y)
+
+        scores = [psum.tile([P, PICKED], F32, name="y%d" % n) for n in range(TILES)]
+        hidden = quantise_hidden(0)
+        for half in range(2):
+            entries = slice(half * HALF // 16, (half + 1) * HALF // 16)
+            cols = slice(half * HALF, (half + 1) * HALF)
+            nc.vector.tensor_copy(v_picked[:, cols], v_table[:].bitcast(U32).indirect(neg_sb[:, entries]))
+            score(scores[0], hidden, cols)
+        for n in range(1, TILES):
+            score(scores[n], quantise_hidden(n), slice(0, PICKED))
 
         exps = []
         for n in range(TILES):

@@ -23,7 +23,7 @@ TILES = PICKED // TILE
 HALF = PICKED // 2
 SPREAD = 8
 V_FIRST = 4
-M_SPLIT = 68
+M_SPLIT = 60
 FLOPS = 2 * 512 * 512 * 512 * 2
 
 
@@ -44,7 +44,7 @@ def tile_picked_zmoco_gelu_p_kernel(tc, x_words, x_scales, w1, v_words, v_scales
         vs_plane = keep.tile([P, PICKED], U8, name="vs_plane", align_bytes=64)
         warm_in = keep.tile([P, 1], F32, name="warm_in")
         warm_out = keep.tile([P, 1], F32, name="warm_out")
-        v_table = late.tile([P, STORED], I32, name="v_table", offset=0, align_bytes=64)
+        v_table = keep.tile([P, STORED], I32, name="v_table", align_bytes=64)
 
         nc.vector.memset(xs_table[:].bitcast(I32), 0)
         nc.gpsimd.memset(warm_in[:], 0.0)
@@ -68,39 +68,43 @@ def tile_picked_zmoco_gelu_p_kernel(tc, x_words, x_scales, w1, v_words, v_scales
             for r in range(4):
                 nc.sync.dma_start(plane[r:P:32, :].bitcast(I32), picked[first + SPREAD * r : P : 32, :].bitcast(I32))
 
-        xs_picked = keep.tile([P, PICKED], U8, name="xs_picked", align_bytes=64)
+        xs_picked = keep.tile([P, PICKED], U8, name="xs_picked", tag="xs_slot", align_bytes=64)
         nc.vector.tensor_copy(xs_picked[:], xs_table[:].indirect(offs_sb[:]))
         place(xs_plane, xs_picked, 0)
         nc.sync.dma_start(v_table[:], v_words[0].rearrange("p n t -> p (n t)").bitcast(I32))
 
-        vs_picked = keep.tile([P, PICKED], U8, name="vs_picked", align_bytes=64)
+        vs_picked = late.tile([P, PICKED], U8, name="vs_picked", offset=0, align_bytes=64)
         nc.vector.tensor_copy(vs_picked[:], vs_table[:].indirect(neg_sb[:]))
         place(vs_plane, vs_picked, V_FIRST)
 
-        w_bf = keep.tile([P, PACK * HIDDEN], BF16, name="w_bf", align_bytes=64)
+        w_bf = keep.tile([P, PACK * HIDDEN], BF16, name="w_bf", tag="w_slot", align_bytes=64)
         w_dst = w_bf[:].rearrange("p (t m j) -> p m t j", t=PACK, j=PACK)
         w_src = w_raw[:].rearrange("p j (m t) -> p m t j", t=PACK)
         nc.vector.tensor_copy(w_dst[:, :M_SPLIT], w_src[:, :M_SPLIT])
         nc.scalar.activation(w_dst[:, M_SPLIT:], w_src[:, M_SPLIT:], ACT.Copy)
 
-        w_codes = keep.tile([P, HIDDEN], U32, name="w_codes", align_bytes=64)
-        w_scale = keep.tile([P, HIDDEN], U8, name="w_scale", align_bytes=64)
-        nc.vector.quantize_mx(w_codes[:].bitcast(FP8X4), w_scale[:], w_bf[:])
-
-        x_picked = keep.tile([P, PICKED], U32, name="x_picked", align_bytes=64)
+        w_codes, w_scale, x_picked = [], [], []
         for half in range(2):
-            cols = slice(half * HALF // 16, (half + 1) * HALF // 16)
-            nc.vector.tensor_copy(x_picked[:, half * HALF : (half + 1) * HALF], x_table[:].bitcast(U32).indirect(offs_sb[:, cols]))
+            codes = keep.tile([P, HIDDEN // 2], U32, name="w_codes%d" % half, align_bytes=64)
+            scale = keep.tile([P, HIDDEN // 2], U8, name="w_scale%d" % half, tag="xs_slot" if half else "w_scale0", align_bytes=64)
+            nc.vector.quantize_mx(codes[:].bitcast(FP8X4), scale[:], w_bf[:, half * 2 * HIDDEN : (half + 1) * 2 * HIDDEN])
+            w_codes.append(codes)
+            w_scale.append(scale)
+        for half in range(2):
+            picked = keep.tile([P, HALF], U32, name="x_picked%d" % half, tag="w_slot" if half else "x_picked0", align_bytes=64)
+            entries = slice(half * HALF // 16, (half + 1) * HALF // 16)
+            nc.vector.tensor_copy(picked[:], x_table[:].bitcast(U32).indirect(offs_sb[:, entries]))
+            x_picked.append(picked)
 
         h_bf = []
         for n in range(TILES):
             pre = psum.tile([P, PACK, TILE], F32, name="pre%d" % n)
-            for j in range(PACK):
+            for j in range(PACK) if n == 0 else reversed(range(PACK)):
                 nc.tensor.matmul_mx(
                     pre[:, j, :],
-                    lhsT=w_codes[:, j * TILE : (j + 1) * TILE].bitcast(FP8X4),
-                    lhsT_scale=w_scale[:, j * TILE : (j + 1) * TILE],
-                    rhs=x_picked[:, n * TILE : (n + 1) * TILE].bitcast(FP8X4),
+                    lhsT=w_codes[j // 2][:, j % 2 * TILE : (j % 2 + 1) * TILE].bitcast(FP8X4),
+                    lhsT_scale=w_scale[j // 2][:, j % 2 * TILE : (j % 2 + 1) * TILE],
+                    rhs=x_picked[n // 2][:, n % 2 * TILE : (n % 2 + 1) * TILE].bitcast(FP8X4),
                     rhs_scale=xs_plane[:, n * TILE : (n + 1) * TILE],
                     start=True,
                     stop=True,
@@ -112,11 +116,11 @@ def tile_picked_zmoco_gelu_p_kernel(tc, x_words, x_scales, w1, v_words, v_scales
         v_picked = keep.tile([P, PICKED], U32, name="v_picked", align_bytes=64)
 
         def quantise_hidden(n):
+            codes = keep.tile([P, TILE], U32, name="h_codes%d" % n, align_bytes=64)
             if n == 0:
-                codes = keep.tile([P, TILE], U32, name="h_codes0", align_bytes=64)
+                scale = keep.tile([P, TILE], U8, name="h_scale0", align_bytes=64)
             else:
-                codes = late.tile([P, TILE], U32, name="h_codes%d" % n, offset=n * TILE * 4, align_bytes=64)
-            scale = keep.tile([P, TILE], U8, name="h_scale%d" % n, align_bytes=64)
+                scale = late.tile([P, TILE], U8, name="h_scale%d" % n, offset=n * TILE, align_bytes=64)
             nc.vector.quantize_mx(codes[:].bitcast(FP8X4), scale[:], h_bf[n][:])
             return codes, scale
 

@@ -117,10 +117,7 @@ def tile_picked_zmoco_gelu_p_kernel(tc, x_words, x_scales, w1, v_words, v_scales
 
         def quantise_hidden(n):
             codes = keep.tile([P, TILE], U32, name="h_codes%d" % n, align_bytes=64)
-            if n == 0:
-                scale = keep.tile([P, TILE], U8, name="h_scale0", align_bytes=64)
-            else:
-                scale = late.tile([P, TILE], U8, name="h_scale%d" % n, offset=n * TILE, align_bytes=64)
+            scale = late.tile([P, TILE], U8, name="h_scale%d" % n, offset=n * TILE, align_bytes=64)
             nc.vector.quantize_mx(codes[:].bitcast(FP8X4), scale[:], h_bf[n][:])
             return codes, scale
 
@@ -137,13 +134,8 @@ def tile_picked_zmoco_gelu_p_kernel(tc, x_words, x_scales, w1, v_words, v_scales
             )
 
         scores = [psum.tile([P, PICKED], F32, name="y%d" % n) for n in range(TILES)]
-        hidden = quantise_hidden(0)
-        for half in range(2):
-            entries = slice(half * HALF // 16, (half + 1) * HALF // 16)
-            cols = slice(half * HALF, (half + 1) * HALF)
-            nc.vector.tensor_copy(v_picked[:, cols], v_table[:].bitcast(U32).indirect(neg_sb[:, entries]))
-            score(scores[0], hidden, cols)
-        for n in range(1, TILES):
+        nc.vector.tensor_copy(v_picked[:], v_table[:].bitcast(U32).indirect(neg_sb[:]))
+        for n in range(TILES):
             score(scores[n], quantise_hidden(n), slice(0, PICKED))
 
         exps = []

@@ -15,6 +15,9 @@ AXIS = mybir.AxisListType
 
 P = 128
 PACK = 4
+QUADRANT = 32
+ROWS_A_QUADRANT = 4
+LIST_ROWS = 16
 STORED = 2048
 PICKED = 512
 HIDDEN = 512
@@ -24,6 +27,7 @@ HALF = PICKED // 2
 SPREAD = 8
 V_FIRST = 4
 M_SPLIT = 60
+LEAD = 128
 FLOPS = 2 * 512 * 512 * 512 * 2
 
 
@@ -31,11 +35,12 @@ def tile_picked_zmoco_gelu_p_kernel(tc, x_words, x_scales, w1, v_words, v_scales
     nc = tc.nc
     with ExitStack() as ctx:
         keep = ctx.enter_context(tc.tile_pool(name="keep", bufs=1))
-        late = ctx.enter_context(tc.tile_pool(name="late", bufs=1))
+        after_x = ctx.enter_context(tc.tile_pool(name="after_x", bufs=1))
+        after_v = ctx.enter_context(tc.tile_pool(name="after_v", bufs=1))
         psum = ctx.enter_context(tc.psum_pool(name="psum", bufs=1))
 
-        offs_sb = keep.tile([P, PICKED // 16], U16, name="offs_sb")
-        neg_sb = keep.tile([P, PICKED // 16], U16, name="neg_sb")
+        offs_sb = keep.tile([P, PICKED // LIST_ROWS], U16, name="offs_sb")
+        neg_sb = keep.tile([P, PICKED // LIST_ROWS], U16, name="neg_sb")
         w_raw = keep.tile([P, PACK, HIDDEN], F32, name="w_raw")
         x_table = keep.tile([P, STORED], I32, name="x_table", align_bytes=64)
         xs_table = keep.tile([P, STORED], U8, name="xs_table", align_bytes=64)
@@ -47,8 +52,8 @@ def tile_picked_zmoco_gelu_p_kernel(tc, x_words, x_scales, w1, v_words, v_scales
         v_table = keep.tile([P, STORED], I32, name="v_table", align_bytes=64)
 
         nc.vector.memset(xs_table[:].bitcast(I32), 0)
-        nc.gpsimd.memset(warm_in[:], 0.0)
         nc.vector.memset(vs_table[:].bitcast(I32), 0)
+        nc.vector.memset(warm_in[:], 0.0)
         nc.vector.memset(xs_plane[:].bitcast(I32), 0)
         nc.vector.memset(vs_plane[:].bitcast(I32), 0)
 
@@ -65,15 +70,15 @@ def tile_picked_zmoco_gelu_p_kernel(tc, x_words, x_scales, w1, v_words, v_scales
         nc.scalar.activation(warm_out[:], warm_in[:], ACT.Gelu_apprx_tanh)
 
         def place(plane, picked, first):
-            for r in range(4):
-                nc.sync.dma_start(plane[r:P:32, :].bitcast(I32), picked[first + SPREAD * r : P : 32, :].bitcast(I32))
+            for r in range(ROWS_A_QUADRANT):
+                nc.sync.dma_start(plane[r:P:QUADRANT, :].bitcast(I32), picked[first + SPREAD * r : P : QUADRANT, :].bitcast(I32))
 
-        xs_picked = keep.tile([P, PICKED], U8, name="xs_picked", tag="xs_slot", align_bytes=64)
+        xs_picked = after_x.tile([P, PICKED], U8, name="xs_picked", offset=0, align_bytes=64)
         nc.vector.tensor_copy(xs_picked[:], xs_table[:].indirect(offs_sb[:]))
         place(xs_plane, xs_picked, 0)
         nc.sync.dma_start(v_table[:], v_words[0].rearrange("p n t -> p (n t)").bitcast(I32))
 
-        vs_picked = late.tile([P, PICKED], U8, name="vs_picked", offset=0, align_bytes=64)
+        vs_picked = after_v.tile([P, PICKED], U8, name="vs_picked", offset=0, align_bytes=64)
         nc.vector.tensor_copy(vs_picked[:], vs_table[:].indirect(neg_sb[:]))
         place(vs_plane, vs_picked, V_FIRST)
 
@@ -83,60 +88,57 @@ def tile_picked_zmoco_gelu_p_kernel(tc, x_words, x_scales, w1, v_words, v_scales
         nc.vector.tensor_copy(w_dst[:, :M_SPLIT], w_src[:, :M_SPLIT])
         nc.scalar.activation(w_dst[:, M_SPLIT:], w_src[:, M_SPLIT:], ACT.Copy)
 
-        w_codes, w_scale, x_picked = [], [], []
-        for half in range(2):
-            codes = keep.tile([P, HIDDEN // 2], U32, name="w_codes%d" % half, align_bytes=64)
-            scale = keep.tile([P, HIDDEN // 2], U8, name="w_scale%d" % half, tag="xs_slot" if half else "w_scale0", align_bytes=64)
-            nc.vector.quantize_mx(codes[:].bitcast(FP8X4), scale[:], w_bf[:, half * 2 * HIDDEN : (half + 1) * 2 * HIDDEN])
-            w_codes.append(codes)
-            w_scale.append(scale)
+        early = PACK // 2
+        w_codes = keep.tile([P, HIDDEN], U32, name="w_codes", align_bytes=64)
+        early_scale = keep.tile([P, early * TILE], U8, name="early_scale", align_bytes=64)
+        nc.vector.quantize_mx(w_codes[:, : early * TILE].bitcast(FP8X4), early_scale[:], w_bf[:, : early * HIDDEN])
+        w_scale = [early_scale[:, t * TILE : (t + 1) * TILE] for t in range(early)]
+        for t in range(early, PACK):
+            late_scale = after_x.tile([P, TILE], U8, name="late_scale%d" % t, offset=(t - early) * TILE, align_bytes=64)
+            nc.vector.quantize_mx(w_codes[:, t * TILE : (t + 1) * TILE].bitcast(FP8X4), late_scale[:], w_bf[:, t * HIDDEN : (t + 1) * HIDDEN])
+            w_scale.append(late_scale[:])
+
+        x_picked = []
         for half in range(2):
             picked = keep.tile([P, HALF], U32, name="x_picked%d" % half, tag="w_slot" if half else "x_picked0", align_bytes=64)
-            entries = slice(half * HALF // 16, (half + 1) * HALF // 16)
+            entries = slice(half * HALF // LIST_ROWS, (half + 1) * HALF // LIST_ROWS)
             nc.vector.tensor_copy(picked[:], x_table[:].bitcast(U32).indirect(offs_sb[:, entries]))
             x_picked.append(picked)
 
         h_bf = []
         for n in range(TILES):
             pre = psum.tile([P, PACK, TILE], F32, name="pre%d" % n)
-            for j in range(PACK) if n == 0 else reversed(range(PACK)):
+            in_half = slice(n % 2 * TILE, (n % 2 + 1) * TILE)
+            for t in range(PACK) if n == 0 else reversed(range(PACK)):
                 nc.tensor.matmul_mx(
-                    pre[:, j, :],
-                    lhsT=w_codes[j // 2][:, j % 2 * TILE : (j % 2 + 1) * TILE].bitcast(FP8X4),
-                    lhsT_scale=w_scale[j // 2][:, j % 2 * TILE : (j % 2 + 1) * TILE],
-                    rhs=x_picked[n // 2][:, n % 2 * TILE : (n % 2 + 1) * TILE].bitcast(FP8X4),
+                    pre[:, t, :],
+                    lhsT=w_codes[:, t * TILE : (t + 1) * TILE].bitcast(FP8X4),
+                    lhsT_scale=w_scale[t],
+                    rhs=x_picked[n // 2][:, in_half].bitcast(FP8X4),
                     rhs_scale=xs_plane[:, n * TILE : (n + 1) * TILE],
                     start=True,
                     stop=True,
                 )
             h = keep.tile([P, TILE * PACK], BF16, name="h_bf%d" % n, align_bytes=64)
-            nc.scalar.activation(h[:].rearrange("p (n j) -> p n j", j=PACK), pre[:].rearrange("p j n -> p n j"), ACT.Gelu_apprx_tanh)
+            nc.scalar.activation(h[:].rearrange("p (s t) -> p s t", t=PACK), pre[:].rearrange("p t s -> p s t"), ACT.Gelu_apprx_tanh)
             h_bf.append(h)
 
         v_picked = keep.tile([P, PICKED], U32, name="v_picked", align_bytes=64)
-
-        def quantise_hidden(n):
-            codes = keep.tile([P, TILE], U32, name="h_codes%d" % n, align_bytes=64)
-            scale = late.tile([P, TILE], U8, name="h_scale%d" % n, offset=n * TILE, align_bytes=64)
-            nc.vector.quantize_mx(codes[:].bitcast(FP8X4), scale[:], h_bf[n][:])
-            return codes, scale
-
-        def score(y, hidden, cols):
-            codes, scale = hidden
-            nc.tensor.matmul_mx(
-                y[:, cols],
-                lhsT=codes[:].bitcast(FP8X4),
-                lhsT_scale=scale[:],
-                rhs=v_picked[:, cols].bitcast(FP8X4),
-                rhs_scale=vs_plane[:, cols],
-                start=True,
-                stop=True,
-            )
-
         scores = [psum.tile([P, PICKED], F32, name="y%d" % n) for n in range(TILES)]
         nc.vector.tensor_copy(v_picked[:], v_table[:].bitcast(U32).indirect(neg_sb[:]))
         for n in range(TILES):
-            score(scores[n], quantise_hidden(n), slice(0, PICKED))
+            h_codes = keep.tile([P, TILE], U32, name="h_codes%d" % n, align_bytes=64)
+            h_scale = after_v.tile([P, TILE], U8, name="h_scale%d" % n, offset=n * TILE, align_bytes=64)
+            nc.vector.quantize_mx(h_codes[:].bitcast(FP8X4), h_scale[:], h_bf[n][:])
+            nc.tensor.matmul_mx(
+                scores[n][:],
+                lhsT=h_codes[:].bitcast(FP8X4),
+                lhsT_scale=h_scale[:],
+                rhs=v_picked[:].bitcast(FP8X4),
+                rhs_scale=vs_plane[:],
+                start=True,
+                stop=True,
+            )
 
         exps = []
         for n in range(TILES):
@@ -147,13 +149,13 @@ def tile_picked_zmoco_gelu_p_kernel(tc, x_words, x_scales, w1, v_words, v_scales
             nc.scalar.activation(e[:], scores[n][:], ACT.Exp, bias=neg_max[:], accum_out=total[:])
             exps.append((e, total))
 
+        cuts = {0: LEAD, TILES - 1: HALF}
         for n in range(TILES):
             e, total = exps[n]
             inv = keep.tile([P, 1], F32, name="inv%d" % n)
             nc.vector.reciprocal(inv[:], total[:])
             res = keep.tile([P, PICKED], F32, name="res%d" % n)
-            pieces = 2 if n in (0, TILES - 1) else 1
-            for piece in range(pieces):
-                cols = slice(piece * PICKED // pieces, (piece + 1) * PICKED // pieces)
+            pieces = (slice(0, cuts[n]), slice(cuts[n], PICKED)) if n in cuts else (slice(0, PICKED),)
+            for cols in pieces:
                 nc.vector.tensor_scalar(res[:, cols], e[:, cols], inv[:], None, ALU.mult)
                 nc.sync.dma_start(out[n * TILE : (n + 1) * TILE, cols], res[:, cols])

@@ -26,7 +26,7 @@ TILES = PICKED // TILE
 HALF = PICKED // 2
 SPREAD = 8
 V_FIRST = 4
-M_SPLIT = 60
+M_SPLIT = 68
 LEAD = 128
 FLOPS = 2 * 512 * 512 * 512 * 2
 

@@ -26,8 +26,9 @@ TILES = PICKED // TILE
 HALF = PICKED // 2
 SPREAD = 8
 V_FIRST = 4
-M_SPLIT = 68
+M_SPLIT = 48
 LEAD = 128
+V_LEAD = 256
 FLOPS = 2 * 512 * 512 * 512 * 2
 
 
@@ -47,27 +48,24 @@ def tile_picked_zmoco_gelu_p_kernel(tc, x_words, x_scales, w1, v_words, v_scales
         vs_table = keep.tile([P, STORED], U8, name="vs_table", align_bytes=64)
         xs_plane = keep.tile([P, PICKED], U8, name="xs_plane", align_bytes=64)
         vs_plane = keep.tile([P, PICKED], U8, name="vs_plane", align_bytes=64)
-        warm_in = keep.tile([P, 1], F32, name="warm_in")
         warm_out = keep.tile([P, 1], F32, name="warm_out")
         v_table = keep.tile([P, STORED], I32, name="v_table", align_bytes=64)
 
         nc.vector.memset(xs_table[:].bitcast(I32), 0)
         nc.vector.memset(vs_table[:].bitcast(I32), 0)
-        nc.vector.memset(warm_in[:], 0.0)
         nc.vector.memset(xs_plane[:].bitcast(I32), 0)
         nc.vector.memset(vs_plane[:].bitcast(I32), 0)
 
         w_rows = w1.rearrange("(p j) c -> p j c", j=PACK)
-        nc.sync.dma_start(w_raw[:, :1], w_rows[:, :1])
+        nc.sync.dma_start(w_raw[:, :2], w_rows[:, :2])
         nc.sync.dma_start(offs_sb[:], offs)
-        nc.sync.dma_start(neg_sb[:], neg)
         nc.sync.dma_start(xs_table[0:P:SPREAD, :].bitcast(I32), x_scales[0].bitcast(I32))
-        nc.sync.dma_start(w_raw[:, 1:2], w_rows[:, 1:2])
-        nc.sync.dma_start(vs_table[V_FIRST:P:SPREAD, :].bitcast(I32), v_scales[0].bitcast(I32))
         nc.sync.dma_start(w_raw[:, 2:], w_rows[:, 2:])
+        nc.sync.dma_start(neg_sb[:], neg)
+        nc.sync.dma_start(vs_table[V_FIRST:P:SPREAD, :].bitcast(I32), v_scales[0].bitcast(I32))
         nc.sync.dma_start(x_table[:], x_words[0].rearrange("p n t -> p (n t)").bitcast(I32))
 
-        nc.scalar.activation(warm_out[:], warm_in[:], ACT.Gelu_apprx_tanh)
+        nc.scalar.activation(warm_out[:], w_raw[:, 0, :1], ACT.Gelu_apprx_tanh)
 
         def place(plane, picked, first):
             for r in range(ROWS_A_QUADRANT):
@@ -75,8 +73,10 @@ def tile_picked_zmoco_gelu_p_kernel(tc, x_words, x_scales, w1, v_words, v_scales
 
         xs_picked = after_x.tile([P, PICKED], U8, name="xs_picked", offset=0, align_bytes=64)
         nc.vector.tensor_copy(xs_picked[:], xs_table[:].indirect(offs_sb[:]))
+        v_rows = v_words[0].rearrange("p n t -> p (n t)").bitcast(I32)
+        nc.sync.dma_start(v_table[:, :V_LEAD], v_rows[:, :V_LEAD])
         place(xs_plane, xs_picked, 0)
-        nc.sync.dma_start(v_table[:], v_words[0].rearrange("p n t -> p (n t)").bitcast(I32))
+        nc.sync.dma_start(v_table[:, V_LEAD:], v_rows[:, V_LEAD:])
 
         vs_picked = after_v.tile([P, PICKED], U8, name="vs_picked", offset=0, align_bytes=64)
         nc.vector.tensor_copy(vs_picked[:], vs_table[:].indirect(neg_sb[:]))

@@ -26,7 +26,7 @@ TILES = PICKED // TILE
 HALF = PICKED // 2
 SPREAD = 8
 V_FIRST = 4
-M_SPLIT = 48
+M_SPLIT = 56
 LEAD = 128
 V_LEAD = 256
 FLOPS = 2 * 512 * 512 * 512 * 2
@@ -83,8 +83,8 @@ def tile_picked_zmoco_gelu_p_kernel(tc, x_words, x_scales, w1, v_words, v_scales
         place(vs_plane, vs_picked, V_FIRST)
 
         w_bf = keep.tile([P, PACK * HIDDEN], BF16, name="w_bf", tag="w_slot", align_bytes=64)
-        w_dst = w_bf[:].rearrange("p (t m j) -> p m t j", t=PACK, j=PACK)
-        w_src = w_raw[:].rearrange("p j (m t) -> p m t j", t=PACK)
+        w_dst = w_bf[:].rearrange("p (t m j) -> p m j t", t=PACK, j=PACK)
+        w_src = w_raw[:].rearrange("p j (m t) -> p m j t", t=PACK)
         nc.vector.tensor_copy(w_dst[:, :M_SPLIT], w_src[:, :M_SPLIT])
         nc.scalar.activation(w_dst[:, M_SPLIT:], w_src[:, M_SPLIT:], ACT.Copy)
 

@@ -29,6 +29,8 @@ V_FIRST = 4
 M_SPLIT = 56
 LEAD = 128
 V_LEAD = 256
+X_PIECES = (128, 128, 128,)
+LINE = 64
 FLOPS = 2 * 512 * 512 * 512 * 2
 
 
@@ -88,7 +90,7 @@ def tile_picked_zmoco_gelu_p_kernel(tc, x_words, x_scales, w1, v_words, v_scales
         nc.vector.tensor_copy(w_dst[:, :M_SPLIT], w_src[:, :M_SPLIT])
         nc.scalar.activation(w_dst[:, M_SPLIT:], w_src[:, M_SPLIT:], ACT.Copy)
 
-        early = PACK // 2
+        early = 3
         w_codes = keep.tile([P, HIDDEN], U32, name="w_codes", align_bytes=64)
         early_scale = keep.tile([P, early * TILE], U8, name="early_scale", align_bytes=64)
         nc.vector.quantize_mx(w_codes[:, : early * TILE].bitcast(FP8X4), early_scale[:], w_bf[:, : early * HIDDEN])
@@ -98,23 +100,27 @@ def tile_picked_zmoco_gelu_p_kernel(tc, x_words, x_scales, w1, v_words, v_scales
             nc.vector.quantize_mx(w_codes[:, t * TILE : (t + 1) * TILE].bitcast(FP8X4), late_scale[:], w_bf[:, t * HIDDEN : (t + 1) * HIDDEN])
             w_scale.append(late_scale[:])
 
-        x_picked = []
-        for half in range(2):
-            picked = keep.tile([P, HALF], U32, name="x_picked%d" % half, tag="w_slot" if half else "x_picked0", align_bytes=64)
-            entries = slice(half * HALF // LIST_ROWS, (half + 1) * HALF // LIST_ROWS)
-            nc.vector.tensor_copy(picked[:], x_table[:].bitcast(U32).indirect(offs_sb[:, entries]))
-            x_picked.append(picked)
+        x_first = keep.tile([P, TILE], U32, name="x_first", align_bytes=64)
+        nc.vector.tensor_copy(x_first[:], x_table[:].bitcast(U32).indirect(offs_sb[:, : TILE // LIST_ROWS]))
+        x_later = after_x.tile([P, PICKED - TILE], U32, name="x_later", offset=PICKED - LINE, align_bytes=64)
+        first = TILE
+        for entries in X_PIECES:
+            nc.vector.tensor_copy(
+                x_later[:, first - TILE : first - TILE + entries],
+                x_table[:].bitcast(U32).indirect(offs_sb[:, first // LIST_ROWS : (first + entries) // LIST_ROWS]),
+            )
+            first = first + entries
+        x_tile = [x_first[:]] + [x_later[:, c : c + TILE] for c in range(0, PICKED - TILE, TILE)]
 
         h_bf = []
         for n in range(TILES):
             pre = psum.tile([P, PACK, TILE], F32, name="pre%d" % n)
-            in_half = slice(n % 2 * TILE, (n % 2 + 1) * TILE)
             for t in range(PACK) if n == 0 else reversed(range(PACK)):
                 nc.tensor.matmul_mx(
                     pre[:, t, :],
                     lhsT=w_codes[:, t * TILE : (t + 1) * TILE].bitcast(FP8X4),
                     lhsT_scale=w_scale[t],
-                    rhs=x_picked[n // 2][:, in_half].bitcast(FP8X4),
+                    rhs=x_tile[n].bitcast(FP8X4),
                     rhs_scale=xs_plane[:, n * TILE : (n + 1) * TILE],
                     start=True,
                     stop=True,

@@ -28,9 +28,12 @@ SPREAD = 8
 V_FIRST = 4
 M_SPLIT = 56
 LEAD = 128
-V_LEAD = 256
+V_LEAD = 0
 X_PIECES = (128, 128, 128,)
 LINE = 64
+W_CUT = 768
+V_PIECES = (512,)
+EARLY_H = 0
 FLOPS = 2 * 512 * 512 * 512 * 2
 
 
@@ -40,11 +43,12 @@ def tile_picked_zmoco_gelu_p_kernel(tc, x_words, x_scales, w1, v_words, v_scales
         keep = ctx.enter_context(tc.tile_pool(name="keep", bufs=1))
         after_x = ctx.enter_context(tc.tile_pool(name="after_x", bufs=1))
         after_v = ctx.enter_context(tc.tile_pool(name="after_v", bufs=1))
+        after_h = ctx.enter_context(tc.tile_pool(name="after_h", bufs=1))
         psum = ctx.enter_context(tc.psum_pool(name="psum", bufs=1))
 
         offs_sb = keep.tile([P, PICKED // LIST_ROWS], U16, name="offs_sb")
         neg_sb = keep.tile([P, PICKED // LIST_ROWS], U16, name="neg_sb")
-        w_raw = keep.tile([P, PACK, HIDDEN], F32, name="w_raw")
+        w_raw = keep.tile([P, PACK * HIDDEN], F32, name="w_raw")
         x_table = keep.tile([P, STORED], I32, name="x_table", align_bytes=64)
         xs_table = keep.tile([P, STORED], U8, name="xs_table", align_bytes=64)
         vs_table = keep.tile([P, STORED], U8, name="vs_table", align_bytes=64)
@@ -58,16 +62,16 @@ def tile_picked_zmoco_gelu_p_kernel(tc, x_words, x_scales, w1, v_words, v_scales
         nc.vector.memset(xs_plane[:].bitcast(I32), 0)
         nc.vector.memset(vs_plane[:].bitcast(I32), 0)
 
-        w_rows = w1.rearrange("(p j) c -> p j c", j=PACK)
-        nc.sync.dma_start(w_raw[:, :2], w_rows[:, :2])
+        w_rows = w1.rearrange("(p j) c -> p (j c)", j=PACK)
+        nc.sync.dma_start(w_raw[:, :W_CUT], w_rows[:, :W_CUT])
         nc.sync.dma_start(offs_sb[:], offs)
         nc.sync.dma_start(xs_table[0:P:SPREAD, :].bitcast(I32), x_scales[0].bitcast(I32))
-        nc.sync.dma_start(w_raw[:, 2:], w_rows[:, 2:])
+        nc.sync.dma_start(w_raw[:, W_CUT:], w_rows[:, W_CUT:])
         nc.sync.dma_start(neg_sb[:], neg)
         nc.sync.dma_start(vs_table[V_FIRST:P:SPREAD, :].bitcast(I32), v_scales[0].bitcast(I32))
         nc.sync.dma_start(x_table[:], x_words[0].rearrange("p n t -> p (n t)").bitcast(I32))
 
-        nc.scalar.activation(warm_out[:], w_raw[:, 0, :1], ACT.Gelu_apprx_tanh)
+        nc.scalar.activation(warm_out[:], w_raw[:, :1], ACT.Gelu_apprx_tanh)
 
         def place(plane, picked, first):
             for r in range(ROWS_A_QUADRANT):
@@ -76,7 +80,6 @@ def tile_picked_zmoco_gelu_p_kernel(tc, x_words, x_scales, w1, v_words, v_scales
         xs_picked = after_x.tile([P, PICKED], U8, name="xs_picked", offset=0, align_bytes=64)
         nc.vector.tensor_copy(xs_picked[:], xs_table[:].indirect(offs_sb[:]))
         v_rows = v_words[0].rearrange("p n t -> p (n t)").bitcast(I32)
-        nc.sync.dma_start(v_table[:, :V_LEAD], v_rows[:, :V_LEAD])
         place(xs_plane, xs_picked, 0)
         nc.sync.dma_start(v_table[:, V_LEAD:], v_rows[:, V_LEAD:])
 
@@ -86,7 +89,7 @@ def tile_picked_zmoco_gelu_p_kernel(tc, x_words, x_scales, w1, v_words, v_scales
 
         w_bf = keep.tile([P, PACK * HIDDEN], BF16, name="w_bf", tag="w_slot", align_bytes=64)
         w_dst = w_bf[:].rearrange("p (t m j) -> p m j t", t=PACK, j=PACK)
-        w_src = w_raw[:].rearrange("p j (m t) -> p m j t", t=PACK)
+        w_src = w_raw[:].rearrange("p (j m t) -> p m j t", t=PACK, j=PACK)
         nc.vector.tensor_copy(w_dst[:, :M_SPLIT], w_src[:, :M_SPLIT])
         nc.scalar.activation(w_dst[:, M_SPLIT:], w_src[:, M_SPLIT:], ACT.Copy)
 
@@ -125,26 +128,48 @@ def tile_picked_zmoco_gelu_p_kernel(tc, x_words, x_scales, w1, v_words, v_scales
                     start=True,
                     stop=True,
                 )
-            h = keep.tile([P, TILE * PACK], BF16, name="h_bf%d" % n, align_bytes=64)
+            h = after_h.tile([P, TILE * PACK], BF16, name="h_bf%d" % n, offset=4 * PICKED * n, align_bytes=64)
             nc.scalar.activation(h[:].rearrange("p (s t) -> p s t", t=PACK), pre[:].rearrange("p t s -> p s t"), ACT.Gelu_apprx_tanh)
             h_bf.append(h)
 
-        v_picked = keep.tile([P, PICKED], U32, name="v_picked", align_bytes=64)
-        scores = [psum.tile([P, PICKED], F32, name="y%d" % n) for n in range(TILES)]
-        nc.vector.tensor_copy(v_picked[:], v_table[:].bitcast(U32).indirect(neg_sb[:]))
-        for n in range(TILES):
+        h_mx = []
+
+        def quantise(n):
             h_codes = keep.tile([P, TILE], U32, name="h_codes%d" % n, align_bytes=64)
-            h_scale = after_v.tile([P, TILE], U8, name="h_scale%d" % n, offset=n * TILE, align_bytes=64)
+            if n < EARLY_H:
+                h_scale = keep.tile([P, TILE], U8, name="h_scale%d" % n, align_bytes=64)
+            else:
+                h_scale = after_v.tile([P, TILE], U8, name="h_scale%d" % n, offset=n * TILE, align_bytes=64)
             nc.vector.quantize_mx(h_codes[:].bitcast(FP8X4), h_scale[:], h_bf[n][:])
-            nc.tensor.matmul_mx(
-                scores[n][:],
-                lhsT=h_codes[:].bitcast(FP8X4),
-                lhsT_scale=h_scale[:],
-                rhs=v_picked[:].bitcast(FP8X4),
-                rhs_scale=vs_plane[:],
-                start=True,
-                stop=True,
+            h_mx.append((h_codes, h_scale))
+
+        for n in range(EARLY_H):
+            quantise(n)
+        v_picked = keep.tile([P, PICKED], U32, name="v_picked", align_bytes=64)
+        v_cols = []
+        first = 0
+        for entries in V_PIECES:
+            nc.vector.tensor_copy(
+                v_picked[:, first : first + entries],
+                v_table[:].bitcast(U32).indirect(neg_sb[:, first // LIST_ROWS : (first + entries) // LIST_ROWS]),
             )
+            v_cols.append(slice(first, first + entries))
+            first = first + entries
+        for n in range(EARLY_H, TILES):
+            quantise(n)
+        scores = [psum.tile([P, PICKED], F32, name="y%d" % n) for n in range(TILES)]
+        for n in range(TILES):
+            h_codes, h_scale = h_mx[n]
+            for cols in v_cols if n == 0 else (slice(0, PICKED),):
+                nc.tensor.matmul_mx(
+                    scores[n][:, cols],
+                    lhsT=h_codes[:].bitcast(FP8X4),
+                    lhsT_scale=h_scale[:],
+                    rhs=v_picked[:, cols].bitcast(FP8X4),
+                    rhs_scale=vs_plane[:, cols],
+                    start=True,
+                    stop=True,
+                )
 
         exps = []
         for n in range(TILES):

@@ -24,8 +24,8 @@ HIDDEN = 512
 TILE = 128
 TILES = PICKED // TILE
 HALF = PICKED // 2
-SPREAD = 8
-V_FIRST = 4
+SPREAD = 4
+SPREAD_FIRST = 32
 M_SPLIT = 56
 LEAD = 128
 V_LEAD = 0
@@ -62,30 +62,32 @@ def tile_picked_zmoco_gelu_p_kernel(tc, x_words, x_scales, w1, v_words, v_scales
         nc.vector.memset(xs_plane[:].bitcast(I32), 0)
         nc.vector.memset(vs_plane[:].bitcast(I32), 0)
 
+        spread_rows = slice(SPREAD_FIRST, SPREAD_FIRST + SPREAD * 16, SPREAD)
         w_rows = w1.rearrange("(p j) c -> p (j c)", j=PACK)
         nc.sync.dma_start(w_raw[:, :W_CUT], w_rows[:, :W_CUT])
         nc.sync.dma_start(offs_sb[:], offs)
-        nc.sync.dma_start(xs_table[0:P:SPREAD, :].bitcast(I32), x_scales[0].bitcast(I32))
+        nc.sync.dma_start(xs_table[spread_rows, :].bitcast(I32), x_scales[0].bitcast(I32))
         nc.sync.dma_start(w_raw[:, W_CUT:], w_rows[:, W_CUT:])
         nc.sync.dma_start(neg_sb[:], neg)
-        nc.sync.dma_start(vs_table[V_FIRST:P:SPREAD, :].bitcast(I32), v_scales[0].bitcast(I32))
+        nc.sync.dma_start(vs_table[spread_rows, :].bitcast(I32), v_scales[0].bitcast(I32))
         nc.sync.dma_start(x_table[:], x_words[0].rearrange("p n t -> p (n t)").bitcast(I32))
 
         nc.scalar.activation(warm_out[:], w_raw[:, :1], ACT.Gelu_apprx_tanh)
 
-        def place(plane, picked, first):
+        def place(plane, picked):
             for r in range(ROWS_A_QUADRANT):
-                nc.sync.dma_start(plane[r:P:QUADRANT, :].bitcast(I32), picked[first + SPREAD * r : P : QUADRANT, :].bitcast(I32))
+                rows = slice(SPREAD_FIRST + SPREAD * r, SPREAD_FIRST + SPREAD * 16, SPREAD * ROWS_A_QUADRANT)
+                nc.sync.dma_start(plane[r:P:QUADRANT, :].bitcast(I32), picked[rows, :].bitcast(I32))
 
         xs_picked = after_x.tile([P, PICKED], U8, name="xs_picked", offset=0, align_bytes=64)
         nc.vector.tensor_copy(xs_picked[:], xs_table[:].indirect(offs_sb[:]))
         v_rows = v_words[0].rearrange("p n t -> p (n t)").bitcast(I32)
-        place(xs_plane, xs_picked, 0)
+        place(xs_plane, xs_picked)
         nc.sync.dma_start(v_table[:, V_LEAD:], v_rows[:, V_LEAD:])
 
         vs_picked = after_v.tile([P, PICKED], U8, name="vs_picked", offset=0, align_bytes=64)
         nc.vector.tensor_copy(vs_picked[:], vs_table[:].indirect(neg_sb[:]))
-        place(vs_plane, vs_picked, V_FIRST)
+        place(vs_plane, vs_picked)
 
         w_bf = keep.tile([P, PACK * HIDDEN], BF16, name="w_bf", tag="w_slot", align_bytes=64)
         w_dst = w_bf[:].rearrange("p (t m j) -> p m j t", t=PACK, j=PACK)

@@ -191,4 +191,5 @@ def tile_picked_zmoco_gelu_p_kernel(tc, x_words, x_scales, w1, v_words, v_scales
             pieces = (slice(0, cuts[n]), slice(cuts[n], PICKED)) if n in cuts else (slice(0, PICKED),)
             for cols in pieces:
                 nc.vector.tensor_scalar(res[:, cols], e[:, cols], inv[:], None, ALU.mult)
-                nc.sync.dma_start(out[n * TILE : (n + 1) * TILE, cols], res[:, cols])
+                queue = nc.scalar if (n, cols.stop) in ((TILES - 2, PICKED), (TILES - 1, PICKED)) else nc.sync
+                queue.dma_start(out[n * TILE : (n + 1) * TILE, cols], res[:, cols])

@@ -28,12 +28,8 @@ SPREAD = 4
 SPREAD_FIRST = 32
 M_SPLIT = 56
 LEAD = 128
-V_LEAD = 0
-X_PIECES = (128, 128, 128,)
 LINE = 64
 W_CUT = 768
-V_PIECES = (512,)
-EARLY_H = 0
 FLOPS = 2 * 512 * 512 * 512 * 2
 
 
@@ -43,19 +39,18 @@ def tile_picked_zmoco_gelu_p_kernel(tc, x_words, x_scales, w1, v_words, v_scales
         keep = ctx.enter_context(tc.tile_pool(name="keep", bufs=1))
         after_x = ctx.enter_context(tc.tile_pool(name="after_x", bufs=1))
         after_v = ctx.enter_context(tc.tile_pool(name="after_v", bufs=1))
-        after_h = ctx.enter_context(tc.tile_pool(name="after_h", bufs=1))
         psum = ctx.enter_context(tc.psum_pool(name="psum", bufs=1))
 
         offs_sb = keep.tile([P, PICKED // LIST_ROWS], U16, name="offs_sb")
         neg_sb = keep.tile([P, PICKED // LIST_ROWS], U16, name="neg_sb")
         w_raw = keep.tile([P, PACK * HIDDEN], F32, name="w_raw")
         x_table = keep.tile([P, STORED], I32, name="x_table", align_bytes=64)
+        v_table = keep.tile([P, STORED], I32, name="v_table", align_bytes=64)
         xs_table = keep.tile([P, STORED], U8, name="xs_table", align_bytes=64)
         vs_table = keep.tile([P, STORED], U8, name="vs_table", align_bytes=64)
         xs_plane = keep.tile([P, PICKED], U8, name="xs_plane", align_bytes=64)
         vs_plane = keep.tile([P, PICKED], U8, name="vs_plane", align_bytes=64)
         warm_out = keep.tile([P, 1], F32, name="warm_out")
-        v_table = keep.tile([P, STORED], I32, name="v_table", align_bytes=64)
 
         nc.vector.memset(xs_table[:].bitcast(I32), 0)
         nc.vector.memset(vs_table[:].bitcast(I32), 0)
@@ -81,40 +76,35 @@ def tile_picked_zmoco_gelu_p_kernel(tc, x_words, x_scales, w1, v_words, v_scales
 
         xs_picked = after_x.tile([P, PICKED], U8, name="xs_picked", offset=0, align_bytes=64)
         nc.vector.tensor_copy(xs_picked[:], xs_table[:].indirect(offs_sb[:]))
-        v_rows = v_words[0].rearrange("p n t -> p (n t)").bitcast(I32)
         place(xs_plane, xs_picked)
-        nc.sync.dma_start(v_table[:, V_LEAD:], v_rows[:, V_LEAD:])
-
-        vs_picked = after_v.tile([P, PICKED], U8, name="vs_picked", offset=0, align_bytes=64)
+        nc.sync.dma_start(v_table[:], v_words[0].rearrange("p n t -> p (n t)").bitcast(I32))
+        vs_picked = after_v.tile([P, PICKED], U8, name="vs_picked", offset=LINE, align_bytes=64)
         nc.vector.tensor_copy(vs_picked[:], vs_table[:].indirect(neg_sb[:]))
         place(vs_plane, vs_picked)
 
-        w_bf = keep.tile([P, PACK * HIDDEN], BF16, name="w_bf", tag="w_slot", align_bytes=64)
+        w_bf = keep.tile([P, PACK * HIDDEN], BF16, name="w_bf", align_bytes=64)
         w_dst = w_bf[:].rearrange("p (t m j) -> p m j t", t=PACK, j=PACK)
         w_src = w_raw[:].rearrange("p (j m t) -> p m j t", t=PACK, j=PACK)
         nc.vector.tensor_copy(w_dst[:, :M_SPLIT], w_src[:, :M_SPLIT])
         nc.scalar.activation(w_dst[:, M_SPLIT:], w_src[:, M_SPLIT:], ACT.Copy)
-
-        early = 3
         w_codes = keep.tile([P, HIDDEN], U32, name="w_codes", align_bytes=64)
-        early_scale = keep.tile([P, early * TILE], U8, name="early_scale", align_bytes=64)
-        nc.vector.quantize_mx(w_codes[:, : early * TILE].bitcast(FP8X4), early_scale[:], w_bf[:, : early * HIDDEN])
-        w_scale = [early_scale[:, t * TILE : (t + 1) * TILE] for t in range(early)]
-        for t in range(early, PACK):
-            late_scale = after_x.tile([P, TILE], U8, name="late_scale%d" % t, offset=(t - early) * TILE, align_bytes=64)
-            nc.vector.quantize_mx(w_codes[:, t * TILE : (t + 1) * TILE].bitcast(FP8X4), late_scale[:], w_bf[:, t * HIDDEN : (t + 1) * HIDDEN])
-            w_scale.append(late_scale[:])
+        w_scale = []
+        for first, last in ((0, 3), (3, 4)):
+            if last == PACK:
+                scale = after_x.tile([P, TILE], U8, name="late_scale", offset=0, align_bytes=64)
+            else:
+                scale = keep.tile([P, (last - first) * TILE], U8, name="w_scale%d" % first, align_bytes=64)
+            nc.vector.quantize_mx(w_codes[:, first * TILE : last * TILE].bitcast(FP8X4), scale[:], w_bf[:, first * HIDDEN : last * HIDDEN])
+            w_scale.extend(scale[:, t * TILE : (t + 1) * TILE] for t in range(last - first))
 
         x_first = keep.tile([P, TILE], U32, name="x_first", align_bytes=64)
         nc.vector.tensor_copy(x_first[:], x_table[:].bitcast(U32).indirect(offs_sb[:, : TILE // LIST_ROWS]))
         x_later = after_x.tile([P, PICKED - TILE], U32, name="x_later", offset=PICKED - LINE, align_bytes=64)
-        first = TILE
-        for entries in X_PIECES:
+        for first in range(TILE, PICKED, TILE):
             nc.vector.tensor_copy(
-                x_later[:, first - TILE : first - TILE + entries],
-                x_table[:].bitcast(U32).indirect(offs_sb[:, first // LIST_ROWS : (first + entries) // LIST_ROWS]),
+                x_later[:, first - TILE : first],
+                x_table[:].bitcast(U32).indirect(offs_sb[:, first // LIST_ROWS : (first + TILE) // LIST_ROWS]),
             )
-            first = first + entries
         x_tile = [x_first[:]] + [x_later[:, c : c + TILE] for c in range(0, PICKED - TILE, TILE)]
 
         h_bf = []
@@ -130,44 +120,36 @@ def tile_picked_zmoco_gelu_p_kernel(tc, x_words, x_scales, w1, v_words, v_scales
                     start=True,
                     stop=True,
                 )
-            h = after_h.tile([P, TILE * PACK], BF16, name="h_bf%d" % n, offset=4 * PICKED * n, align_bytes=64)
+            h = keep.tile([P, TILE * PACK], BF16, name="h_bf%d" % n, align_bytes=64)
             nc.scalar.activation(h[:].rearrange("p (s t) -> p s t", t=PACK), pre[:].rearrange("p t s -> p s t"), ACT.Gelu_apprx_tanh)
             h_bf.append(h)
 
+        scores = [psum.tile([P, PICKED], F32, name="y%d" % n) for n in range(TILES)]
         h_mx = []
 
         def quantise(n):
             h_codes = keep.tile([P, TILE], U32, name="h_codes%d" % n, align_bytes=64)
-            if n < EARLY_H:
-                h_scale = keep.tile([P, TILE], U8, name="h_scale%d" % n, align_bytes=64)
-            else:
-                h_scale = after_v.tile([P, TILE], U8, name="h_scale%d" % n, offset=n * TILE, align_bytes=64)
+            h_scale = after_v.tile([P, TILE], U8, name="h_scale%d" % n, offset=n * TILE, align_bytes=64)
             nc.vector.quantize_mx(h_codes[:].bitcast(FP8X4), h_scale[:], h_bf[n][:])
             h_mx.append((h_codes, h_scale))
 
-        for n in range(EARLY_H):
+        v_first = keep.tile([P, HALF], U32, name="v_first", align_bytes=64)
+        nc.vector.tensor_copy(v_first[:], v_table[:].bitcast(U32).indirect(neg_sb[:, : HALF // LIST_ROWS]))
+        quantise(0)
+        v_second = after_v.tile([P, HALF], U32, name="v_second", offset=TILES * TILE, align_bytes=64)
+        nc.vector.tensor_copy(v_second[:], v_table[:].bitcast(U32).indirect(neg_sb[:, HALF // LIST_ROWS :]))
+        for n in range(1, TILES):
             quantise(n)
-        v_picked = keep.tile([P, PICKED], U32, name="v_picked", align_bytes=64)
-        v_cols = []
-        first = 0
-        for entries in V_PIECES:
-            nc.vector.tensor_copy(
-                v_picked[:, first : first + entries],
-                v_table[:].bitcast(U32).indirect(neg_sb[:, first // LIST_ROWS : (first + entries) // LIST_ROWS]),
-            )
-            v_cols.append(slice(first, first + entries))
-            first = first + entries
-        for n in range(EARLY_H, TILES):
-            quantise(n)
-        scores = [psum.tile([P, PICKED], F32, name="y%d" % n) for n in range(TILES)]
+
         for n in range(TILES):
             h_codes, h_scale = h_mx[n]
-            for cols in v_cols if n == 0 else (slice(0, PICKED),):
+            for half, v_picked in enumerate((v_first, v_second)):
+                cols = slice(half * HALF, (half + 1) * HALF)
                 nc.tensor.matmul_mx(
                     scores[n][:, cols],
                     lhsT=h_codes[:].bitcast(FP8X4),
                     lhsT_scale=h_scale[:],
-                    rhs=v_picked[:, cols].bitcast(FP8X4),
+                    rhs=v_picked[:].bitcast(FP8X4),
                     rhs_scale=vs_plane[:, cols],
                     start=True,
                     stop=True,
@@ -180,11 +162,11 @@ def tile_picked_zmoco_gelu_p_kernel(tc, x_words, x_scales, w1, v_words, v_scales
             e = keep.tile([P, PICKED], F32, name="e%d" % n)
             total = keep.tile([P, 1], F32, name="total%d" % n)
             nc.scalar.activation(e[:], scores[n][:], ACT.Exp, bias=neg_max[:], accum_out=total[:])
-            exps.append((e, total))
+            exps.append((e, total, neg_max))
 
         cuts = {0: LEAD, TILES - 1: HALF}
         for n in range(TILES):
-            e, total = exps[n]
+            e, total, neg_max = exps[n]
             inv = keep.tile([P, 1], F32, name="inv%d" % n)
             nc.vector.reciprocal(inv[:], total[:])
             res = keep.tile([P, PICKED], F32, name="res%d" % n)

@@ -26,10 +26,10 @@ TILES = PICKED // TILE
 HALF = PICKED // 2
 SPREAD = 4
 SPREAD_FIRST = 32
-M_SPLIT = 56
+M_SPLIT = 48
 LEAD = 128
 LINE = 64
-W_CUT = 768
+W_CUT = 640
 FLOPS = 2 * 512 * 512 * 512 * 2
 
 
@@ -61,9 +61,9 @@ def tile_picked_zmoco_gelu_p_kernel(tc, x_words, x_scales, w1, v_words, v_scales
         w_rows = w1.rearrange("(p j) c -> p (j c)", j=PACK)
         nc.sync.dma_start(w_raw[:, :W_CUT], w_rows[:, :W_CUT])
         nc.sync.dma_start(offs_sb[:], offs)
+        nc.sync.dma_start(neg_sb[:], neg)
         nc.sync.dma_start(xs_table[spread_rows, :].bitcast(I32), x_scales[0].bitcast(I32))
         nc.sync.dma_start(w_raw[:, W_CUT:], w_rows[:, W_CUT:])
-        nc.sync.dma_start(neg_sb[:], neg)
         nc.sync.dma_start(vs_table[spread_rows, :].bitcast(I32), v_scales[0].bitcast(I32))
         nc.sync.dma_start(x_table[:], x_words[0].rearrange("p n t -> p (n t)").bitcast(I32))
 
@@ -85,8 +85,9 @@ def tile_picked_zmoco_gelu_p_kernel(tc, x_words, x_scales, w1, v_words, v_scales
         w_bf = keep.tile([P, PACK * HIDDEN], BF16, name="w_bf", align_bytes=64)
         w_dst = w_bf[:].rearrange("p (t m j) -> p m j t", t=PACK, j=PACK)
         w_src = w_raw[:].rearrange("p (j m t) -> p m j t", t=PACK, j=PACK)
-        nc.vector.tensor_copy(w_dst[:, :M_SPLIT], w_src[:, :M_SPLIT])
-        nc.scalar.activation(w_dst[:, M_SPLIT:], w_src[:, M_SPLIT:], ACT.Copy)
+        nc.vector.tensor_copy(w_dst[:, :M_SPLIT, :, :3], w_src[:, :M_SPLIT, :, :3])
+        nc.scalar.activation(w_dst[:, M_SPLIT:, :, :3], w_src[:, M_SPLIT:, :, :3], ACT.Copy)
+        nc.scalar.activation(w_dst[:, :, :, 3], w_src[:, :, :, 3], ACT.Copy)
         w_codes = keep.tile([P, HIDDEN], U32, name="w_codes", align_bytes=64)
         w_scale = []
         for first, last in ((0, 3), (3, 4)):
@@ -97,15 +98,18 @@ def tile_picked_zmoco_gelu_p_kernel(tc, x_words, x_scales, w1, v_words, v_scales
             nc.vector.quantize_mx(w_codes[:, first * TILE : last * TILE].bitcast(FP8X4), scale[:], w_bf[:, first * HIDDEN : last * HIDDEN])
             w_scale.extend(scale[:, t * TILE : (t + 1) * TILE] for t in range(last - first))
 
-        x_first = keep.tile([P, TILE], U32, name="x_first", align_bytes=64)
-        nc.vector.tensor_copy(x_first[:], x_table[:].bitcast(U32).indirect(offs_sb[:, : TILE // LIST_ROWS]))
-        x_later = after_x.tile([P, PICKED - TILE], U32, name="x_later", offset=PICKED - LINE, align_bytes=64)
-        for first in range(TILE, PICKED, TILE):
+        x_tile = []
+        for n in range(2):
+            picked = keep.tile([P, TILE], U32, name="x_first%d" % n, align_bytes=64)
+            nc.vector.tensor_copy(picked[:], x_table[:].bitcast(U32).indirect(offs_sb[:, n * TILE // LIST_ROWS : (n + 1) * TILE // LIST_ROWS]))
+            x_tile.append(picked[:])
+        x_later = after_x.tile([P, HALF], U32, name="x_later", offset=PICKED - LINE, align_bytes=64)
+        for first in range(HALF, PICKED, TILE):
             nc.vector.tensor_copy(
-                x_later[:, first - TILE : first],
+                x_later[:, first - HALF : first - HALF + TILE],
                 x_table[:].bitcast(U32).indirect(offs_sb[:, first // LIST_ROWS : (first + TILE) // LIST_ROWS]),
             )
-        x_tile = [x_first[:]] + [x_later[:, c : c + TILE] for c in range(0, PICKED - TILE, TILE)]
+            x_tile.append(x_later[:, first - HALF : first - HALF + TILE])
 
         h_bf = []
         for n in range(TILES):

from contextlib import ExitStack

import concourse.mybir as mybir

F32 = mybir.dt.float32
BF16 = mybir.dt.bfloat16
I32 = mybir.dt.int32
U32 = mybir.dt.uint32
U16 = mybir.dt.uint16
U8 = mybir.dt.uint8
FP8X4 = mybir.dt.float8_e4m3fn_x4
ACT = mybir.ActivationFunctionType
ALU = mybir.AluOpType
AXIS = mybir.AxisListType

P = 128
PACK = 4
QUADRANT = 32
ROWS_A_QUADRANT = 4
LIST_ROWS = 16
STORED = 2048
PICKED = 512
HIDDEN = 512
TILE = 128
TILES = PICKED // TILE
HALF = PICKED // 2
SPREAD = 4
SPREAD_FIRST = 32
M_SPLIT = 48
LEAD = 128
LINE = 64
W_CUT = 640
FLOPS = 2 * 512 * 512 * 512 * 2


def tile_picked_zmoco_gelu_p_kernel(tc, x_words, x_scales, w1, v_words, v_scales, offs, neg, out):
    nc = tc.nc
    with ExitStack() as ctx:
        keep = ctx.enter_context(tc.tile_pool(name="keep", bufs=1))
        after_x = ctx.enter_context(tc.tile_pool(name="after_x", bufs=1))
        after_v = ctx.enter_context(tc.tile_pool(name="after_v", bufs=1))
        psum = ctx.enter_context(tc.psum_pool(name="psum", bufs=1))

        offs_sb = keep.tile([P, PICKED // LIST_ROWS], U16, name="offs_sb")
        neg_sb = keep.tile([P, PICKED // LIST_ROWS], U16, name="neg_sb")
        w_raw = keep.tile([P, PACK * HIDDEN], F32, name="w_raw")
        x_table = keep.tile([P, STORED], I32, name="x_table", align_bytes=64)
        v_table = keep.tile([P, STORED], I32, name="v_table", align_bytes=64)
        xs_table = keep.tile([P, STORED], U8, name="xs_table", align_bytes=64)
        vs_table = keep.tile([P, STORED], U8, name="vs_table", align_bytes=64)
        xs_plane = keep.tile([P, PICKED], U8, name="xs_plane", align_bytes=64)
        vs_plane = keep.tile([P, PICKED], U8, name="vs_plane", align_bytes=64)
        warm_out = keep.tile([P, 1], F32, name="warm_out")

        nc.vector.memset(xs_table[:].bitcast(I32), 0)
        nc.vector.memset(vs_table[:].bitcast(I32), 0)
        nc.vector.memset(xs_plane[:].bitcast(I32), 0)
        nc.vector.memset(vs_plane[:].bitcast(I32), 0)

        spread_rows = slice(SPREAD_FIRST, SPREAD_FIRST + SPREAD * 16, SPREAD)
        w_rows = w1.rearrange("(p j) c -> p (j c)", j=PACK)
        nc.sync.dma_start(w_raw[:, :W_CUT], w_rows[:, :W_CUT])
        nc.sync.dma_start(offs_sb[:], offs)
        nc.sync.dma_start(neg_sb[:], neg)
        nc.sync.dma_start(xs_table[spread_rows, :].bitcast(I32), x_scales[0].bitcast(I32))
        nc.sync.dma_start(w_raw[:, W_CUT:], w_rows[:, W_CUT:])
        nc.sync.dma_start(vs_table[spread_rows, :].bitcast(I32), v_scales[0].bitcast(I32))
        nc.sync.dma_start(x_table[:], x_words[0].rearrange("p n t -> p (n t)").bitcast(I32))

        nc.scalar.activation(warm_out[:], w_raw[:, :1], ACT.Gelu_apprx_tanh)

        def place(plane, picked):
            for r in range(ROWS_A_QUADRANT):
                rows = slice(SPREAD_FIRST + SPREAD * r, SPREAD_FIRST + SPREAD * 16, SPREAD * ROWS_A_QUADRANT)
                nc.sync.dma_start(plane[r:P:QUADRANT, :].bitcast(I32), picked[rows, :].bitcast(I32))

        xs_picked = after_x.tile([P, PICKED], U8, name="xs_picked", offset=0, align_bytes=64)
        nc.vector.tensor_copy(xs_picked[:], xs_table[:].indirect(offs_sb[:]))
        place(xs_plane, xs_picked)
        nc.sync.dma_start(v_table[:], v_words[0].rearrange("p n t -> p (n t)").bitcast(I32))
        vs_picked = after_v.tile([P, PICKED], U8, name="vs_picked", offset=LINE, align_bytes=64)
        nc.vector.tensor_copy(vs_picked[:], vs_table[:].indirect(neg_sb[:]))
        place(vs_plane, vs_picked)

        w_bf = keep.tile([P, PACK * HIDDEN], BF16, name="w_bf", align_bytes=64)
        w_dst = w_bf[:].rearrange("p (t m j) -> p m j t", t=PACK, j=PACK)
        w_src = w_raw[:].rearrange("p (j m t) -> p m j t", t=PACK, j=PACK)
        nc.vector.tensor_copy(w_dst[:, :M_SPLIT, :, :3], w_src[:, :M_SPLIT, :, :3])
        nc.scalar.activation(w_dst[:, M_SPLIT:, :, :3], w_src[:, M_SPLIT:, :, :3], ACT.Copy)
        nc.scalar.activation(w_dst[:, :, :, 3], w_src[:, :, :, 3], ACT.Copy)
        w_codes = keep.tile([P, HIDDEN], U32, name="w_codes", align_bytes=64)
        w_scale = []
        for first, last in ((0, 3), (3, 4)):
            if last == PACK:
                scale = after_x.tile([P, TILE], U8, name="late_scale", offset=0, align_bytes=64)
            else:
                scale = keep.tile([P, (last - first) * TILE], U8, name="w_scale%d" % first, align_bytes=64)
            nc.vector.quantize_mx(w_codes[:, first * TILE : last * TILE].bitcast(FP8X4), scale[:], w_bf[:, first * HIDDEN : last * HIDDEN])
            w_scale.extend(scale[:, t * TILE : (t + 1) * TILE] for t in range(last - first))

        x_tile = []
        for n in range(2):
            picked = keep.tile([P, TILE], U32, name="x_first%d" % n, align_bytes=64)
            nc.vector.tensor_copy(picked[:], x_table[:].bitcast(U32).indirect(offs_sb[:, n * TILE // LIST_ROWS : (n + 1) * TILE // LIST_ROWS]))
            x_tile.append(picked[:])
        x_later = after_x.tile([P, HALF], U32, name="x_later", offset=PICKED - LINE, align_bytes=64)
        for first in range(HALF, PICKED, TILE):
            nc.vector.tensor_copy(
                x_later[:, first - HALF : first - HALF + TILE],
                x_table[:].bitcast(U32).indirect(offs_sb[:, first // LIST_ROWS : (first + TILE) // LIST_ROWS]),
            )
            x_tile.append(x_later[:, first - HALF : first - HALF + TILE])

        h_bf = []
        for n in range(TILES):
            pre = psum.tile([P, PACK, TILE], F32, name="pre%d" % n)
            for t in range(PACK) if n == 0 else reversed(range(PACK)):
                nc.tensor.matmul_mx(
                    pre[:, t, :],
                    lhsT=w_codes[:, t * TILE : (t + 1) * TILE].bitcast(FP8X4),
                    lhsT_scale=w_scale[t],
                    rhs=x_tile[n].bitcast(FP8X4),
                    rhs_scale=xs_plane[:, n * TILE : (n + 1) * TILE],
                    start=True,
                    stop=True,
                )
            h = keep.tile([P, TILE * PACK], BF16, name="h_bf%d" % n, align_bytes=64)
            nc.scalar.activation(h[:].rearrange("p (s t) -> p s t", t=PACK), pre[:].rearrange("p t s -> p s t"), ACT.Gelu_apprx_tanh)
            h_bf.append(h)

        scores = [psum.tile([P, PICKED], F32, name="y%d" % n) for n in range(TILES)]
        h_mx = []

        def quantise(n):
            h_codes = keep.tile([P, TILE], U32, name="h_codes%d" % n, align_bytes=64)
            h_scale = after_v.tile([P, TILE], U8, name="h_scale%d" % n, offset=n * TILE, align_bytes=64)
            nc.vector.quantize_mx(h_codes[:].bitcast(FP8X4), h_scale[:], h_bf[n][:])
            h_mx.append((h_codes, h_scale))

        v_first = keep.tile([P, HALF], U32, name="v_first", align_bytes=64)
        nc.vector.tensor_copy(v_first[:], v_table[:].bitcast(U32).indirect(neg_sb[:, : HALF // LIST_ROWS]))
        quantise(0)
        v_second = after_v.tile([P, HALF], U32, name="v_second", offset=TILES * TILE, align_bytes=64)
        nc.vector.tensor_copy(v_second[:], v_table[:].bitcast(U32).indirect(neg_sb[:, HALF // LIST_ROWS :]))
        for n in range(1, TILES):
            quantise(n)

        for n in range(TILES):
            h_codes, h_scale = h_mx[n]
            for half, v_picked in enumerate((v_first, v_second)):
                cols = slice(half * HALF, (half + 1) * HALF)
                nc.tensor.matmul_mx(
                    scores[n][:, cols],
                    lhsT=h_codes[:].bitcast(FP8X4),
                    lhsT_scale=h_scale[:],
                    rhs=v_picked[:].bitcast(FP8X4),
                    rhs_scale=vs_plane[:, cols],
                    start=True,
                    stop=True,
                )

        exps = []
        for n in range(TILES):
            neg_max = keep.tile([P, 1], F32, name="neg_max%d" % n)
            nc.vector.tensor_reduce(neg_max[:], scores[n][:], AXIS.X, ALU.max, negate=True)
            e = keep.tile([P, PICKED], F32, name="e%d" % n)
            total = keep.tile([P, 1], F32, name="total%d" % n)
            nc.scalar.activation(e[:], scores[n][:], ACT.Exp, bias=neg_max[:], accum_out=total[:])
            exps.append((e, total, neg_max))

        cuts = {0: LEAD, TILES - 1: HALF}
        for n in range(TILES):
            e, total, neg_max = exps[n]
            inv = keep.tile([P, 1], F32, name="inv%d" % n)
            nc.vector.reciprocal(inv[:], total[:])
            res = keep.tile([P, PICKED], F32, name="res%d" % n)
            pieces = (slice(0, cuts[n]), slice(cuts[n], PICKED)) if n in cuts else (slice(0, PICKED),)
            for cols in pieces:
                nc.vector.tensor_scalar(res[:, cols], e[:, cols], inv[:], None, ALU.mult)
                queue = nc.scalar if (n, cols.stop) in ((TILES - 2, PICKED), (TILES - 1, PICKED)) else nc.sync
                queue.dma_start(out[n * TILE : (n + 1) * TILE, cols], res[:, cols])
